import numpy as np
import ml_dtypes


def mxq(x, axis, fmt="e4m3"):
    dtype, down = {"e4m3": (ml_dtypes.float8_e4m3fn, 7), "e5m2": (ml_dtypes.float8_e5m2, 14)}[fmt]
    v = np.moveaxis(np.asarray(x, np.float32).astype(ml_dtypes.bfloat16).astype(np.float64), axis, -1)
    blocks = v.reshape(v.shape[:-1] + (-1, 32))
    amax = np.abs(blocks).max(-1, keepdims=True)
    byte = np.maximum(np.where(amax > 0, np.frexp(amax)[1] - 1 + 127, 0) - down, 1)
    scale = np.exp2(byte - 127.0)
    codes = (blocks / scale).astype(np.float32).astype(dtype).astype(np.float64)
    return np.moveaxis((codes * scale).reshape(v.shape), -1, axis)


WIDE = False


def mx_kscale(k):
    if not WIDE:
        return np.ones(k)
    levels = np.array([10, -10, 5, -5, 0])
    if k % 512:
        return np.exp2(np.random.permutation(np.resize(levels, k // 32))).repeat(32)
    a = np.empty((k // 512, 16))
    for p in range(k // 512):
        a[p, :8] = np.random.permutation(np.resize(levels, 8))
        for g in range(8):
            far = levels[np.abs(levels - a[p, g]) >= 10]
            a[p, g + 8] = far[np.random.randint(len(far))]
    return np.exp2(a.ravel()).repeat(32)


def f64(x):
    return np.asarray(x).astype(np.float64)


def striped(idx):
    return np.tile(idx.reshape(-1, 16).T, (8, 1)).astype(np.uint16)


def unstriped(offs):
    return offs[:16].T.reshape(-1).astype(np.int64)


def striped8(idx):
    return np.concatenate([x.reshape(-1, 16).T for x in idx]).astype(np.uint16)


def runs(offs, k):
    lists = np.stack([offs[16 * r : 16 * r + 16].T.reshape(-1) for r in range(8)]).astype(np.int64)
    return lists[np.arange(k) % 512 // 64]


def pack_weight(w):
    k, n = w.shape
    w = f64(np.asarray(w, np.float32).astype(ml_dtypes.bfloat16)).reshape(k // 32, 32, n)
    amax = np.abs(w).max(1)
    byte = np.clip(np.where(amax > 0, np.frexp(amax)[1] - 1 + 127 - 7, 1), 1, 254)
    scaled = (w * np.exp2(127.0 - byte)[:, None, :]).reshape(k, n).astype(np.float32)
    words = np.ascontiguousarray(scaled.reshape(k // 512, 128, 4, n).transpose(0, 1, 3, 2)).astype(ml_dtypes.float8_e4m3fn).view(np.uint8)
    return words, np.ascontiguousarray(byte.astype(np.uint8).reshape(k // 512, 16, n))


def unpack_weight(words, scales):
    g, p, n, _ = words.shape
    vals = np.ascontiguousarray(words).view(ml_dtypes.float8_e4m3fn).astype(np.float64) * np.repeat(np.exp2(scales.astype(np.float64) - 127.0), 8, axis=1)[..., None]
    return vals.transpose(0, 1, 3, 2).reshape(g * 512, n)


def sigmoid(v):
    return 1.0 / (1.0 + np.exp(-np.maximum(v, -700.0)))

def planes(y):
    n, m = y.shape
    v = y.astype(np.float32).astype(ml_dtypes.bfloat16).astype(np.float64).reshape(n // 32, 32, m)
    top = np.abs(v).max(1)
    byte = np.clip(np.where(top > 0, np.frexp(top)[1] - 1 + 127 - 7, 1), 1, 254)
    codes = (v * np.exp2(127.0 - byte)[:, None, :]).reshape(n, m).astype(np.float32).astype(ml_dtypes.float8_e4m3fn).view(np.uint8)
    words = codes.reshape(n // 512, 128, 4, m).transpose(0, 1, 3, 2)
    return np.ascontiguousarray(words), np.ascontiguousarray(byte.astype(np.uint8).reshape(n // 512, 16, m))


K, T, S, N, H = 512, 2048, 512, 512, 512


def setup_inputs():
    n = np.random.standard_normal
    s = mx_kscale(K)[:, None]
    u = mx_kscale(S)
    packed_xT = pack_weight(n((K, T)) * s)
    packed_w1 = pack_weight(n((S, N)) / np.sqrt(S) / u[:, None])
    return {
        "x_words": packed_xT[0],
        "x_scales": packed_xT[1],
        "wa": (n((K, H)) / np.sqrt(K) / s).astype(np.float32),
        "wb": (n((K, H)) / np.sqrt(K) / s).astype(np.float32),
        "sl": np.random.uniform(1.0, 2.0, (S, 1)).astype(np.float32),
        "th": (0.5 * n((S, 1))).astype(np.float32),
        "gt": (np.random.uniform(0.5, 1.5, (S, 1)) * u[:, None]).astype(np.float32),
        "w1_words": packed_w1[0],
        "w1_scales": packed_w1[1],
        "offs": striped(np.random.permutation(T)[:S]),
        "two": striped(np.random.permutation(T)[:S]),
        "n1": striped8(np.stack([np.random.permutation(H) for _ in range(8)])),
        "n2": striped8(np.stack([np.random.permutation(H) for _ in range(8)])),
        "n3": striped8(np.stack([np.random.permutation(H) for _ in range(8)])),
        "n4": striped8(np.stack([np.random.permutation(H) for _ in range(8)])),
    }


def reference(x_words, x_scales, wa, wb, sl, th, gt, w1_words, w1_scales, offs, two, n1, n2, n3, n4):
    xq = unpack_weight(x_words, x_scales)[:, unstriped(offs)]
    y = xq.T @ mxq(f64(wa), 0, "e4m3")
    x_two = unpack_weight(x_words, x_scales)[:, unstriped(two)]
    d = x_two.T @ mxq(f64(wb), 0, "e4m3")
    sg = sigmoid(f64(sl) * (d[np.arange(S)[:, None], runs(n1, S)] - f64(th)))
    z = f64(gt) * (np.maximum(y * sg, d[np.arange(S)[:, None], runs(n2, S)] - d))
    h = unpack_weight(w1_words, w1_scales).T @ mxq(z, 0, "e4m3")
    pa = h[np.arange(N)[:, None], runs(n3, N)]
    pb = h[np.arange(N)[:, None], runs(n4, N)]
    mu = 0.3125 * (h + pa + pb)
    out_0 = (h - mu) / (np.sqrt((pa - mu) ** 2 + (pb - mu) ** 2 + 0.25))
    return (out_0,) + planes(out_0)

@@ -1,0 +1,270 @@
+import math
+from contextlib import ExitStack
+
+import concourse.mybir as mybir
+from concourse.masks import make_identity
+
+K, T, S, H, N = 512, 2048, 512, 512, 512
+FLOPS = 3 * 2 * 512 * 512 * 512
+
+F32 = mybir.dt.float32
+BF16 = mybir.dt.bfloat16
+I32 = mybir.dt.int32
+U32 = mybir.dt.uint32
+U16 = mybir.dt.uint16
+U8 = mybir.dt.uint8
+FP8X4 = mybir.dt.float8_e4m3fn_x4
+ALU = mybir.AluOpType
+ACT = mybir.ActivationFunctionType
+
+P = 128
+PACK = 4
+HALF = 256
+MIX_CHUNKS = ((0, 256), (256, 256))
+OUT_CHUNKS = ((0, 256), (256, 256))
+FETCH = 0.6
+
+
+def weave(dst, src):
+    return (
+        dst.rearrange("p (c i t) -> p c t i", i=4, t=PACK),
+        src.rearrange("p t (c i) -> p c t i", i=4),
+    )
+
+
+def entries(lst, c0, n):
+    return lst[:, c0 // 16 : (c0 + n) // 16]
+
+
+def tile_picked_twtmxbstd_none_po_kernel(
+    tc, x_words, x_scales, wa, wb, sl, th, gt, w1_words, w1_scales, offs, two, n1, n2, n3, n4, out_0, out_1, out_2
+):
+    nc = tc.nc
+    with ExitStack() as ctx:
+        keep = ctx.enter_context(tc.tile_pool(name="keep", bufs=1))
+        ring = ctx.enter_context(tc.tile_pool(name="ring", bufs=4))
+        psum = ctx.enter_context(tc.psum_pool(name="psum", bufs=1))
+
+        def load_list(src, name):
+            lst = keep.tile([P, S // 16], U16, name=name)
+            nc.sync.dma_start(lst[:], src)
+            return lst
+
+        def load_scale_rows(plane, src):
+            for q in range(4):
+                nc.sync.dma_start(
+                    out=plane[32 * q : 32 * q + 4, :].bitcast(I32),
+                    in_=src[0, 4 * q : 4 * q + 4, :].bitcast(I32),
+                )
+
+        def load_column(src, name):
+            col = keep.tile([P, PACK], F32, name=name)
+            nc.sync.dma_start(out=col[:], in_=src.rearrange("(p t) o -> p (t o)", t=PACK))
+            return col
+
+        def load_weight_half(w, half, name):
+            raw = keep.tile([P, PACK, HALF], F32, name=name)
+            nc.sync.dma_start(
+                out=raw[:], in_=w.rearrange("(p j) c -> p j c", j=PACK)[:, :, half * HALF : (half + 1) * HALF]
+            )
+            return raw
+
+        xs = keep.tile([P, T], U8, name="xs", align_bytes=64)
+        w1s_raw = keep.tile([P, N], U8, name="w1s_raw", align_bytes=64)
+        nc.vector.memset(w1s_raw[:].bitcast(I32), 0)
+        two_l = load_list(two, "two_l")
+        for q in range(4):
+            nc.sync.dma_start(
+                out=xs[32 * q : 32 * q + 32, :].bitcast(I32),
+                in_=x_scales[0, 4 * q : 4 * q + 4, :].bitcast(I32).partition_broadcast(8),
+            )
+        offs_l = load_list(offs, "offs_l")
+        xw = keep.tile([P, T], U32, name="xw", align_bytes=64)
+        nc.sync.dma_start(out=xw[:].bitcast(I32), in_=x_words[0].rearrange("p n t -> p (n t)").bitcast(I32))
+        wb_raw = [load_weight_half(wb, half, "wb_raw%d" % half) for half in range(2)]
+        n1_l = load_list(n1, "n1_l")
+        sl_c = load_column(sl, "sl_c")
+        th_c = load_column(th, "th_c")
+        n2_l = load_list(n2, "n2_l")
+        w1w_raw = keep.tile([P, N], U32, name="w1w_raw", align_bytes=64)
+        nc.sync.dma_start(out=w1w_raw[:].bitcast(I32), in_=w1_words[0].rearrange("p n t -> p (n t)").bitcast(I32))
+        wa_raw = [load_weight_half(wa, half, "wa_raw%d" % half) for half in range(2)]
+        gt_c = load_column(gt, "gt_c")
+        load_scale_rows(w1s_raw, w1_scales)
+        n3_l = load_list(n3, "n3_l")
+        n4_l = load_list(n4, "n4_l")
+        ident = keep.tile([P, P], F32, name="ident")
+        make_identity(nc, ident[:])
+
+        def pick(window, lst, dtype, name):
+            got = keep.tile([P, S], dtype, name=name, align_bytes=64)
+            nc.vector.tensor_copy(got[:].rearrange("p (t m) -> p m t", t=PACK), window[:].indirect(lst[:]))
+            return got
+
+        def quantise_weight(raws, copy, name):
+            codes = keep.tile([P, H], U32, name=name + "_codes", align_bytes=64)
+            plane = keep.tile([P, H], U8, name=name + "_plane", align_bytes=64)
+            for half in range(2):
+                woven = keep.tile([P, PACK * HALF], BF16, name=name + "_woven%d" % half, align_bytes=64)
+                copy(*weave(woven[:], raws[half][:]))
+                cols = slice(half * HALF, (half + 1) * HALF)
+                nc.vector.quantize_mx(out=codes[:, cols].bitcast(FP8X4), scales=plane[:, cols], in_=woven[:])
+            return codes, plane
+
+        def product(bank, lhs_codes, lhs_plane, t, rhs_codes, rhs_plane):
+            cols = slice(t * P, (t + 1) * P)
+            nc.tensor.matmul_mx(
+                out=bank,
+                lhsT=lhs_codes[:, cols].bitcast(FP8X4),
+                lhsT_scale=lhs_plane[:, cols],
+                rhs=rhs_codes.bitcast(FP8X4),
+                rhs_scale=rhs_plane,
+                start=True,
+                stop=True,
+            )
+
+        two_s = pick(xs, two_l, U8, "two_s")
+        offs_s = pick(xs, offs_l, U8, "offs_s")
+        two_w = pick(xw, two_l, U32, "two_w")
+        wb_codes, wb_plane = quantise_weight(wb_raw, nc.scalar.copy, "wb")
+        d_ps = [psum.tile([P, H], F32, name="d_ps%d" % t, tag="bank%d" % t) for t in range(PACK)]
+        d_sb = [keep.tile([P, H], F32, name="d_sb%d" % t) for t in range(PACK)]
+        for t in range(PACK):
+            product(d_ps[t][:], two_w, two_s, t, wb_codes[:], wb_plane[:])
+        offs_w = pick(xw, offs_l, U32, "offs_w")
+
+        w1w = keep.tile([P, N], U32, name="w1w", align_bytes=64)
+        nc.scalar.copy(w1w[:].rearrange("p (t m) -> p t m", t=PACK), w1w_raw[:].rearrange("p (m t) -> p t m", t=PACK))
+        neg_b = keep.tile([P, PACK], F32, name="neg_b")
+        nc.vector.scalar_tensor_tensor(neg_b[:], sl_c[:], -1.0, th_c[:], ALU.mult, ALU.mult)
+
+        wa_codes, wa_plane = quantise_weight(wa_raw, nc.vector.tensor_copy, "wa")
+        y_ps = [psum.tile([P, H], F32, name="y_ps%d" % t, tag="bank%d" % (PACK + t)) for t in range(PACK)]
+        for t in range(PACK):
+            product(y_ps[t][:], offs_w, offs_s, t, wa_codes[:], wa_plane[:])
+        w1s = keep.tile([P, N], U8, name="w1s", align_bytes=64)
+        nc.vector.tensor_copy(
+            w1s[:].rearrange("p (t m) -> p t m", t=PACK), w1s_raw[:].rearrange("p (m t) -> p t m", t=PACK)
+        )
+
+        h_ps = []
+        h_sb = [keep.tile([P, H], F32, name="h_sb%d" % t) for t in range(PACK)]
+        for ci, (c0, n) in enumerate(MIX_CHUNKS):
+            cols = slice(c0, c0 + n)
+            z_rows = keep.tile([P, PACK, n], BF16, name="z_rows%d" % ci)
+            larger = []
+            for t in range(PACK):
+                if ci == 0:
+                    nc.scalar.copy(d_sb[t][:], d_ps[t][:])
+                sg = ring.tile([P, n], F32, name="sg")
+                nc.scalar.activation(
+                    sg[:], d_sb[t][:].indirect(entries(n1_l, c0, n)), ACT.Sigmoid,
+                    bias=neg_b[:, t : t + 1], scale=sl_c[:, t : t + 1],
+                )
+                d2 = ring.tile([P, n], F32, name="d2")
+                nc.scalar.activation(d2[:], d_sb[t][:].indirect(entries(n2_l, c0, n)), ACT.Copy)
+                gated = ring.tile([P, n], F32, name="gated")
+                nc.vector.tensor_tensor(gated[:], y_ps[t][:, cols], sg[:], ALU.mult)
+                if t > 0:
+                    nc.vector.tensor_scalar_mul(z_rows[:, t - 1, :], larger[t - 1][:], gt_c[:, t - 1 : t])
+                diff = ring.tile([P, n], F32, name="diff")
+                nc.vector.tensor_tensor(diff[:], d2[:], d_sb[t][:, cols], ALU.subtract)
+                big = ring.tile([P, n], F32, name="big")
+                nc.vector.tensor_tensor(big[:], gated[:], diff[:], ALU.max)
+                larger.append(big)
+            nc.vector.tensor_scalar_mul(z_rows[:, PACK - 1, :], larger[PACK - 1][:], gt_c[:, PACK - 1 : PACK])
+            z_woven = keep.tile([P, PACK * n], BF16, name="z_woven%d" % ci, align_bytes=64)
+            nc.vector.tensor_copy(*weave(z_woven[:], z_rows[:]))
+            z_codes = keep.tile([P, n], U32, name="z_codes%d" % ci, align_bytes=64)
+            z_plane = keep.tile([P, n], U8, name="z_plane%d" % ci, align_bytes=64)
+            nc.vector.quantize_mx(out=z_codes[:].bitcast(FP8X4), scales=z_plane[:], in_=z_woven[:])
+            for t in range(PACK):
+                if ci == 0:
+                    h_ps.append(psum.tile([P, H], F32, name="h_ps%d" % t, tag="bank%d" % t))
+                product(h_ps[t][:, cols], w1w, w1s, t, z_codes[:], z_plane[:])
+            for t in range(PACK):
+                nc.scalar.copy(h_sb[t][:, cols], h_ps[t][:, cols])
+
+        out_rows = out_0.rearrange("(p t) j -> p t j", t=PACK)
+        o_codes = keep.tile([P, H], U32, name="o_codes", align_bytes=64)
+        o_plane = keep.tile([P, H], U8, name="o_plane", align_bytes=64)
+        o_words = out_1[0].rearrange("p n t -> p (n t)").bitcast(I32)
+        results = [keep.tile([P, PACK, n], F32, name="result%d" % ci) for ci, (c0, n) in enumerate(OUT_CHUNKS)]
+        units = [(ci, t) for ci in range(len(OUT_CHUNKS)) for t in range(PACK)]
+        held = {}
+
+        def add_turned(bank, first, second, n):
+            for b in range(n // P):
+                blk = slice(b * P, (b + 1) * P)
+                nc.tensor.matmul(bank[:, blk], first[:, blk], ident[:], start=True, stop=False, is_transpose=True)
+                nc.tensor.matmul(bank[:, blk], second[:, blk], ident[:], start=False, stop=True, is_transpose=True)
+
+        def fetch(u):
+            ci, t = units[u]
+            c0, n = OUT_CHUNKS[ci]
+            pa = ring.tile([P, n], F32, name="pa")
+            nc.scalar.activation(pa[:], h_sb[t][:].indirect(entries(n3_l, c0, n)), ACT.Copy, scale=FETCH)
+            pb = ring.tile([P, n], F32, name="pb")
+            nc.vector.tensor_scalar(pb[:], h_sb[t][:].indirect(entries(n4_l, c0, n)), -FETCH, 0.0, ALU.mult, ALU.add)
+            held[u] = dict(pa=pa, pb=pb)
+
+        def both(u):
+            ci, t = units[u]
+            c0, n = OUT_CHUNKS[ci]
+            pair = ring.tile([P, n], F32, name="pair")
+            nc.vector.tensor_tensor(pair[:], held[u]["pb"][:], held[u]["pa"][:], ALU.subtract)
+            held[u]["pair"] = pair
+
+        def numerator(u):
+            ci, t = units[u]
+            c0, n = OUT_CHUNKS[ci]
+            num = ring.tile([P, n], F32, name="num", bufs=5)
+            nc.vector.scalar_tensor_tensor(
+                num[:], held[u]["pair"][:], 5.0 / 11.0 / FETCH, h_sb[t][:, c0 : c0 + n], ALU.mult, ALU.add
+            )
+            held[u]["num"] = num
+
+        def squares(u):
+            ci, t = units[u]
+            c0, n = OUT_CHUNKS[ci]
+            turned = psum.tile([P, 2, n], F32, name="turned", tag="bank%d" % ((PACK + u) % 8))
+            add_turned(turned[:, 0, :], held[u]["pa"], held[u]["pb"], n)
+            add_turned(turned[:, 1, :], h_sb[t][:, c0 : c0 + n], held[u]["pair"], n)
+            sq = ring.tile([P, 2, n], F32, name="sq")
+            nc.scalar.activation(sq[:, 0, :], turned[:, 0, :], ACT.Square, scale=math.sqrt(0.5) / FETCH)
+            nc.scalar.activation(sq[:, 1, :], turned[:, 1, :], ACT.Square, scale=math.sqrt(0.5) * 0.625)
+            held[u]["sq"] = sq
+
+        def inverse_root(u):
+            ci, t = units[u]
+            c0, n = OUT_CHUNKS[ci]
+            total = psum.tile([P, n], F32, name="total", tag="bank%d" % (u % 8))
+            add_turned(total, held[u]["sq"][:, 0, :], held[u]["sq"][:, 1, :], n)
+            root = ring.tile([P, n], F32, name="root")
+            nc.scalar.activation(root[:], total[:], ACT.Abs_reciprocal_sqrt, bias=0.25)
+            held[u]["root"] = root
+
+        def finish(u):
+            ci, t = units[u]
+            c0, n = OUT_CHUNKS[ci]
+            cols = slice(c0, c0 + n)
+            nc.vector.scalar_tensor_tensor(
+                results[ci][:, t, :], held[u]["num"][:], 0.6875, held[u]["root"][:], ALU.mult, ALU.mult
+            )
+            nc.sync.dma_start(out=out_rows[:, t, cols], in_=results[ci][:, t, :])
+            if t == PACK - 1:
+                o_woven = keep.tile([P, PACK * n], BF16, name="o_woven%d" % ci, align_bytes=64)
+                nc.vector.tensor_copy(*weave(o_woven[:], results[ci][:]))
+                nc.vector.quantize_mx(out=o_codes[:, cols].bitcast(FP8X4), scales=o_plane[:, cols], in_=o_woven[:])
+                nc.sync.dma_start(out=o_words[:, cols], in_=o_codes[:, cols].bitcast(I32))
+
+        steps = ((fetch, 0), (both, 1), (finish, 3), (numerator, 1), (squares, 1), (inverse_root, 2))
+        for i in range(len(units) + 4):
+            for step, lag in steps:
+                if 0 <= i - lag < len(units):
+                    step(i - lag)
+        for q in range(4):
+            queue = nc.sync if q % 2 == 0 else nc.scalar
+            queue.dma_start(
+                out=out_2[0, 4 * q : 4 * q + 4, :].bitcast(I32), in_=o_plane[32 * q : 32 * q + 4, :].bitcast(I32)
+            )

@@ -20,9 +20,33 @@ ACT = mybir.ActivationFunctionType
 P = 128
 PACK = 4
 HALF = 256
-MIX_CHUNKS = ((0, 256), (256, 256))
-OUT_CHUNKS = ((0, 256), (256, 256))
+MIX_CHUNKS = ((0,256,),(256,256,),)
+OUT_CHUNKS = ((0,256,),(256,256,),)
 FETCH = 0.6
+WARM = 0
+ORDER = "wb x n1 sl th n2 wa w1 gt w1s n3 n4"
+WB_ENG = "vv"
+EARLY = 1
+FB = 4
+MB = 5
+SUB = 0
+OSUB = 1
+MLAGS = (1,2,2,3,)
+PB_ENG = "vvvvvvvv"
+W1_LATE = 0
+WB_SPLIT = 1
+WA_SPLIT = 2
+WA_ENG = "vv"
+D_ENG = "ssss"
+D2_ENG = "vvssssss"
+GT_ENG = "vvvvvvvv"
+ZW_ENG = "vvv"
+H_ENG = "ssssvsvs"
+PA_ENG = "ssssssss"
+MODE = "pppvppvp"
+OW_ENG = "vvs"
+W1_ENG = "s"
+LAGS = (1,6,4,2,4,)
 
 
 def weave(dst, src):
@@ -62,12 +86,40 @@ def tile_picked_twtmxbstd_none_po_kernel(
             nc.sync.dma_start(out=col[:], in_=src.rearrange("(p t) o -> p (t o)", t=PACK))
             return col
 
-        def load_weight_half(w, half, name):
-            raw = keep.tile([P, PACK, HALF], F32, name=name)
-            nc.sync.dma_start(
-                out=raw[:], in_=w.rearrange("(p j) c -> p j c", j=PACK)[:, :, half * HALF : (half + 1) * HALF]
-            )
-            return raw
+        def load_weight(w, split, name):
+            view = w.rearrange("(p j) c -> p j c", j=PACK)
+            if split == 1:
+                raw = keep.tile([P, PACK, H], F32, name=name)
+                nc.sync.dma_start(out=raw[:], in_=view)
+                return [raw[:, :, :HALF], raw[:, :, HALF:]]
+            raws = []
+            for half in range(2):
+                raw = keep.tile([P, PACK, HALF], F32, name=name + str(half))
+                nc.sync.dma_start(out=raw[:], in_=view[:, :, half * HALF : (half + 1) * HALF])
+                raws.append(raw[:])
+            return raws
+
+        def copy_on(eng, dst, src):
+            if eng == "s":
+                nc.scalar.copy(dst, src)
+            else:
+                nc.vector.tensor_copy(dst, src)
+
+        def weave_on(eng, dst, src, n):
+            if eng == "b":
+                nc.scalar.copy(*weave(dst[:, : n], src[:, :, : n // 4]))
+                nc.vector.tensor_copy(*weave(dst[:, n :], src[:, :, n // 4 :]))
+            elif eng == "h":
+                nc.scalar.copy(*weave(dst[:, : 2 * n], src[:, :, : n // 2]))
+                nc.vector.tensor_copy(*weave(dst[:, 2 * n :], src[:, :, n // 2 :]))
+            else:
+                copy_on(eng, *weave(dst, src))
+
+        def gather_on(eng, dst, src, scale):
+            if eng == "s":
+                nc.scalar.activation(dst, src, ACT.Copy, scale=scale)
+            else:
+                nc.vector.tensor_scalar(dst, src, scale, 0.0, ALU.mult, ALU.add)
 
         xs = keep.tile([P, T], U8, name="xs", align_bytes=64)
         w1s_raw = keep.tile([P, N], U8, name="w1s_raw", align_bytes=64)
@@ -79,34 +131,46 @@ def tile_picked_twtmxbstd_none_po_kernel(
                 in_=x_scales[0, 4 * q : 4 * q + 4, :].bitcast(I32).partition_broadcast(8),
             )
         offs_l = load_list(offs, "offs_l")
-        xw = keep.tile([P, T], U32, name="xw", align_bytes=64)
-        nc.sync.dma_start(out=xw[:].bitcast(I32), in_=x_words[0].rearrange("p n t -> p (n t)").bitcast(I32))
-        wb_raw = [load_weight_half(wb, half, "wb_raw%d" % half) for half in range(2)]
-        n1_l = load_list(n1, "n1_l")
-        sl_c = load_column(sl, "sl_c")
-        th_c = load_column(th, "th_c")
-        n2_l = load_list(n2, "n2_l")
-        w1w_raw = keep.tile([P, N], U32, name="w1w_raw", align_bytes=64)
-        nc.sync.dma_start(out=w1w_raw[:].bitcast(I32), in_=w1_words[0].rearrange("p n t -> p (n t)").bitcast(I32))
-        wa_raw = [load_weight_half(wa, half, "wa_raw%d" % half) for half in range(2)]
-        gt_c = load_column(gt, "gt_c")
-        load_scale_rows(w1s_raw, w1_scales)
-        n3_l = load_list(n3, "n3_l")
-        n4_l = load_list(n4, "n4_l")
+        got = {}
+
+        def load_words(src, width, name):
+            words = keep.tile([P, width], U32, name=name, align_bytes=64)
+            nc.sync.dma_start(out=words[:].bitcast(I32), in_=src[0].rearrange("p n t -> p (n t)").bitcast(I32))
+            return words
+
+        for key in ORDER.split():
+            if key == "x":
+                xw = load_words(x_words, T, "xw")
+            elif key == "wb":
+                wb_raw = load_weight(wb, WB_SPLIT, "wb_raw")
+            elif key == "wa":
+                wa_raw = load_weight(wa, WA_SPLIT, "wa_raw")
+            elif key == "w1":
+                w1w_raw = load_words(w1_words, N, "w1w_raw")
+            elif key == "w1s":
+                load_scale_rows(w1s_raw, w1_scales)
+            elif key in ("sl", "th", "gt"):
+                got[key] = load_column(dict(sl=sl, th=th, gt=gt)[key], key + "_c")
+            else:
+                got[key] = load_list(dict(n1=n1, n2=n2, n3=n3, n4=n4)[key], key + "_l")
+        sl_c, th_c, gt_c = got["sl"], got["th"], got["gt"]
+        n1_l, n2_l, n3_l, n4_l = got["n1"], got["n2"], got["n3"], got["n4"]
         ident = keep.tile([P, P], F32, name="ident")
         make_identity(nc, ident[:])
+        if WARM:
+            warm = keep.tile([P, 2], F32, name="warm")
 
         def pick(window, lst, dtype, name):
             got = keep.tile([P, S], dtype, name=name, align_bytes=64)
             nc.vector.tensor_copy(got[:].rearrange("p (t m) -> p m t", t=PACK), window[:].indirect(lst[:]))
             return got
 
-        def quantise_weight(raws, copy, name):
+        def quantise_weight(raws, engs, name):
             codes = keep.tile([P, H], U32, name=name + "_codes", align_bytes=64)
             plane = keep.tile([P, H], U8, name=name + "_plane", align_bytes=64)
             for half in range(2):
                 woven = keep.tile([P, PACK * HALF], BF16, name=name + "_woven%d" % half, align_bytes=64)
-                copy(*weave(woven[:], raws[half][:]))
+                weave_on(engs[half], woven[:], raws[half], HALF)
                 cols = slice(half * HALF, (half + 1) * HALF)
                 nc.vector.quantize_mx(out=codes[:, cols].bitcast(FP8X4), scales=plane[:, cols], in_=woven[:])
             return codes, plane
@@ -125,23 +189,23 @@ def tile_picked_twtmxbstd_none_po_kernel(
 
         two_s = pick(xs, two_l, U8, "two_s")
         offs_s = pick(xs, offs_l, U8, "offs_s")
+        wb_codes, wb_plane = quantise_weight(wb_raw, WB_ENG, "wb")
         two_w = pick(xw, two_l, U32, "two_w")
-        wb_codes, wb_plane = quantise_weight(wb_raw, nc.scalar.copy, "wb")
         d_ps = [psum.tile([P, H], F32, name="d_ps%d" % t, tag="bank%d" % t) for t in range(PACK)]
         d_sb = [keep.tile([P, H], F32, name="d_sb%d" % t) for t in range(PACK)]
         for t in range(PACK):
             product(d_ps[t][:], two_w, two_s, t, wb_codes[:], wb_plane[:])
         offs_w = pick(xw, offs_l, U32, "offs_w")
 
-        w1w = keep.tile([P, N], U32, name="w1w", align_bytes=64)
-        nc.scalar.copy(w1w[:].rearrange("p (t m) -> p t m", t=PACK), w1w_raw[:].rearrange("p (m t) -> p t m", t=PACK))
         neg_b = keep.tile([P, PACK], F32, name="neg_b")
         nc.vector.scalar_tensor_tensor(neg_b[:], sl_c[:], -1.0, th_c[:], ALU.mult, ALU.mult)
 
-        wa_codes, wa_plane = quantise_weight(wa_raw, nc.vector.tensor_copy, "wa")
+        wa_codes, wa_plane = quantise_weight(wa_raw, WA_ENG, "wa")
         y_ps = [psum.tile([P, H], F32, name="y_ps%d" % t, tag="bank%d" % (PACK + t)) for t in range(PACK)]
         for t in range(PACK):
             product(y_ps[t][:], offs_w, offs_s, t, wa_codes[:], wa_plane[:])
+        w1w = keep.tile([P, N], U32, name="w1w", align_bytes=64)
+        copy_on(W1_ENG, w1w[:].rearrange("p (t m) -> p t m", t=PACK), w1w_raw[:].rearrange("p (m t) -> p t m", t=PACK))
         w1s = keep.tile([P, N], U8, name="w1s", align_bytes=64)
         nc.vector.tensor_copy(
             w1s[:].rearrange("p (t m) -> p t m", t=PACK), w1s_raw[:].rearrange("p (m t) -> p t m", t=PACK)
@@ -149,41 +213,84 @@ def tile_picked_twtmxbstd_none_po_kernel(
 
         h_ps = []
         h_sb = [keep.tile([P, H], F32, name="h_sb%d" % t) for t in range(PACK)]
-        for ci, (c0, n) in enumerate(MIX_CHUNKS):
-            cols = slice(c0, c0 + n)
-            z_rows = keep.tile([P, PACK, n], BF16, name="z_rows%d" % ci)
-            larger = []
-            for t in range(PACK):
+        mix_units = [(ci, t) for ci in range(len(MIX_CHUNKS)) for t in range(PACK)]
+        z_rows = [keep.tile([P, PACK, n], BF16, name="z_rows%d" % ci) for ci, (c0, n) in enumerate(MIX_CHUNKS)]
+        mixed = {}
+
+        def look_up(u):
+            ci, t = mix_units[u]
+            c0, n = MIX_CHUNKS[ci]
+            if ci == 0:
+                copy_on(D_ENG[t], d_sb[t][:], d_ps[t][:])
+            sg = ring.tile([P, n], F32, name="sg", bufs=MB)
+            nc.scalar.activation(
+                sg[:], d_sb[t][:].indirect(entries(n1_l, c0, n)), ACT.Sigmoid,
+                bias=neg_b[:, t : t + 1], scale=sl_c[:, t : t + 1],
+            )
+            d2 = ring.tile([P, n], F32, name="d2", bufs=MB)
+            gather_on(D2_ENG[u], d2[:], d_sb[t][:].indirect(entries(n2_l, c0, n)), 1.0)
+            if WARM and u == len(mix_units) - 1:
+                nc.scalar.activation(warm[:, 1:2], sg[:, 0:1], ACT.Abs_reciprocal_sqrt, bias=0.25)
+            mixed[u] = dict(sg=sg, d2=d2)
+
+        def candidates(u):
+            ci, t = mix_units[u]
+            c0, n = MIX_CHUNKS[ci]
+            diff = ring.tile([P, n], F32, name="diff")
+            nc.vector.tensor_tensor(diff[:], mixed[u]["d2"][:], d_sb[t][:, c0 : c0 + n], ALU.subtract)
+            gated = ring.tile([P, n], F32, name="gated")
+            nc.vector.tensor_tensor(gated[:], y_ps[t][:, c0 : c0 + n], mixed[u]["sg"][:], ALU.mult)
+            mixed[u]["diff"], mixed[u]["gated"] = diff, gated
+
+        def larger(u):
+            ci, t = mix_units[u]
+            big = ring.tile([P, MIX_CHUNKS[ci][1]], F32, name="big")
+            nc.vector.tensor_tensor(big[:], mixed[u]["gated"][:], mixed[u]["diff"][:], ALU.max)
+            mixed[u]["big"] = big
+
+        def weigh(u):
+            ci, t = mix_units[u]
+            if GT_ENG[u] == "v":
+                nc.vector.tensor_scalar_mul(z_rows[ci][:, t, :], mixed[u]["big"][:], gt_c[:, t : t + 1])
+            else:
+                nc.scalar.activation(z_rows[ci][:, t, :], mixed[u]["big"][:], ACT.Copy, scale=gt_c[:, t : t + 1])
+
+        woven_z = {}
+
+        def pieces(ci, chunks, sub):
+            c0, n = chunks[ci]
+            w = P if (sub and ci == len(chunks) - 1) else n
+            return [(k, w) for k in range(0, n, w)]
+
+        def weave_z(u):
+            ci, t = mix_units[u]
+            if t == PACK - 1:
+                for k, w in pieces(ci, MIX_CHUNKS, SUB):
+                    zw = keep.tile([P, PACK * w], BF16, name="z_woven%d_%d" % (ci, k), align_bytes=64)
+                    weave_on(ZW_ENG[ci + k // w], zw[:], z_rows[ci][:, :, k : k + w], w)
+                    woven_z[ci, k] = zw
+
+        def mix_product(u):
+            ci, t = mix_units[u]
+            if t == PACK - 1:
                 if ci == 0:
-                    nc.scalar.copy(d_sb[t][:], d_ps[t][:])
-                sg = ring.tile([P, n], F32, name="sg")
-                nc.scalar.activation(
-                    sg[:], d_sb[t][:].indirect(entries(n1_l, c0, n)), ACT.Sigmoid,
-                    bias=neg_b[:, t : t + 1], scale=sl_c[:, t : t + 1],
-                )
-                d2 = ring.tile([P, n], F32, name="d2")
-                nc.scalar.activation(d2[:], d_sb[t][:].indirect(entries(n2_l, c0, n)), ACT.Copy)
-                gated = ring.tile([P, n], F32, name="gated")
-                nc.vector.tensor_tensor(gated[:], y_ps[t][:, cols], sg[:], ALU.mult)
-                if t > 0:
-                    nc.vector.tensor_scalar_mul(z_rows[:, t - 1, :], larger[t - 1][:], gt_c[:, t - 1 : t])
-                diff = ring.tile([P, n], F32, name="diff")
-                nc.vector.tensor_tensor(diff[:], d2[:], d_sb[t][:, cols], ALU.subtract)
-                big = ring.tile([P, n], F32, name="big")
-                nc.vector.tensor_tensor(big[:], gated[:], diff[:], ALU.max)
-                larger.append(big)
-            nc.vector.tensor_scalar_mul(z_rows[:, PACK - 1, :], larger[PACK - 1][:], gt_c[:, PACK - 1 : PACK])
-            z_woven = keep.tile([P, PACK * n], BF16, name="z_woven%d" % ci, align_bytes=64)
-            nc.vector.tensor_copy(*weave(z_woven[:], z_rows[:]))
-            z_codes = keep.tile([P, n], U32, name="z_codes%d" % ci, align_bytes=64)
-            z_plane = keep.tile([P, n], U8, name="z_plane%d" % ci, align_bytes=64)
-            nc.vector.quantize_mx(out=z_codes[:].bitcast(FP8X4), scales=z_plane[:], in_=z_woven[:])
-            for t in range(PACK):
-                if ci == 0:
-                    h_ps.append(psum.tile([P, H], F32, name="h_ps%d" % t, tag="bank%d" % t))
-                product(h_ps[t][:, cols], w1w, w1s, t, z_codes[:], z_plane[:])
-            for t in range(PACK):
-                nc.scalar.copy(h_sb[t][:, cols], h_ps[t][:, cols])
+                    for j in range(PACK):
+                        h_ps.append(psum.tile([P, H], F32, name="h_ps%d" % j, tag="bank%d" % j))
+                c0, n = MIX_CHUNKS[ci]
+                for k, w in pieces(ci, MIX_CHUNKS, SUB):
+                    z_codes = keep.tile([P, w], U32, name="z_codes%d_%d" % (ci, k), align_bytes=64)
+                    z_plane = keep.tile([P, w], U8, name="z_plane%d_%d" % (ci, k), align_bytes=64)
+                    nc.vector.quantize_mx(out=z_codes[:].bitcast(FP8X4), scales=z_plane[:], in_=woven_z[ci, k][:])
+                    for j in range(PACK):
+                        product(h_ps[j][:, c0 + k : c0 + k + w], w1w, w1s, j, z_codes[:], z_plane[:])
+                for j in range(PACK):
+                    copy_on(H_ENG[4 * ci + j], h_sb[j][:, c0 : c0 + n], h_ps[j][:, c0 : c0 + n])
+
+        steps = ((look_up, 0), (candidates, 0), (mix_product, MLAGS[3]), (larger, MLAGS[0]), (weigh, MLAGS[1]), (weave_z, MLAGS[2]))
+        for i in range(len(mix_units) + max(MLAGS)):
+            for step, lag in steps:
+                if 0 <= i - lag < len(mix_units):
+                    step(i - lag)
 
         out_rows = out_0.rearrange("(p t) j -> p t j", t=PACK)
         o_codes = keep.tile([P, H], U32, name="o_codes", align_bytes=64)
@@ -202,10 +309,10 @@ def tile_picked_twtmxbstd_none_po_kernel(
         def fetch(u):
             ci, t = units[u]
             c0, n = OUT_CHUNKS[ci]
-            pa = ring.tile([P, n], F32, name="pa")
-            nc.scalar.activation(pa[:], h_sb[t][:].indirect(entries(n3_l, c0, n)), ACT.Copy, scale=FETCH)
-            pb = ring.tile([P, n], F32, name="pb")
-            nc.vector.tensor_scalar(pb[:], h_sb[t][:].indirect(entries(n4_l, c0, n)), -FETCH, 0.0, ALU.mult, ALU.add)
+            pa = ring.tile([P, n], F32, name="pa", bufs=FB)
+            gather_on(PA_ENG[u], pa[:], h_sb[t][:].indirect(entries(n3_l, c0, n)), FETCH)
+            pb = ring.tile([P, n], F32, name="pb", bufs=FB)
+            gather_on(PB_ENG[u], pb[:], h_sb[t][:].indirect(entries(n4_l, c0, n)), -FETCH)
             held[u] = dict(pa=pa, pb=pb)
 
         def both(u):
@@ -218,7 +325,7 @@ def tile_picked_twtmxbstd_none_po_kernel(
         def numerator(u):
             ci, t = units[u]
             c0, n = OUT_CHUNKS[ci]
-            num = ring.tile([P, n], F32, name="num", bufs=5)
+            num = ring.tile([P, n], F32, name="num", bufs=6)
             nc.vector.scalar_tensor_tensor(
                 num[:], held[u]["pair"][:], 5.0 / 11.0 / FETCH, h_sb[t][:, c0 : c0 + n], ALU.mult, ALU.add
             )
@@ -227,9 +334,27 @@ def tile_picked_twtmxbstd_none_po_kernel(
         def squares(u):
             ci, t = units[u]
             c0, n = OUT_CHUNKS[ci]
+            if MODE[u] == "v":
+                forms = ring.tile([P, 2, n], F32, name="forms")
+                nc.vector.tensor_tensor(forms[:, 0, :], held[u]["pa"][:], held[u]["pb"][:], ALU.add)
+                nc.vector.tensor_tensor(forms[:, 1, :], h_sb[t][:, c0 : c0 + n], held[u]["pair"][:], ALU.add)
+                sq = ring.tile([P, 2, n], F32, name="sq")
+                nc.scalar.activation(sq[:], forms[:], ACT.Square)
+                held[u]["sq"] = sq
+                return
             turned = psum.tile([P, 2, n], F32, name="turned", tag="bank%d" % ((PACK + u) % 8))
-            add_turned(turned[:, 0, :], held[u]["pa"], held[u]["pb"], n)
-            add_turned(turned[:, 1, :], h_sb[t][:, c0 : c0 + n], held[u]["pair"], n)
+            if EARLY:
+                terms = ((1, h_sb[t][:, c0 : c0 + n]), (0, held[u]["pa"]), (0, held[u]["pb"]), (1, held[u]["pair"]))
+                passes = [(half, src, b) for half, src in terms for b in range(n // P)]
+                for k, (half, src, b) in enumerate(passes):
+                    blk = slice(b * P, (b + 1) * P)
+                    nc.tensor.matmul(
+                        turned[:, half, blk], src[:, blk], ident[:],
+                        start=(k == 0), stop=(k == len(passes) - 1), is_transpose=True,
+                    )
+            else:
+                add_turned(turned[:, 0, :], held[u]["pa"], held[u]["pb"], n)
+                add_turned(turned[:, 1, :], h_sb[t][:, c0 : c0 + n], held[u]["pair"], n)
             sq = ring.tile([P, 2, n], F32, name="sq")
             nc.scalar.activation(sq[:, 0, :], turned[:, 0, :], ACT.Square, scale=math.sqrt(0.5) / FETCH)
             nc.scalar.activation(sq[:, 1, :], turned[:, 1, :], ACT.Square, scale=math.sqrt(0.5) * 0.625)
@@ -238,6 +363,15 @@ def tile_picked_twtmxbstd_none_po_kernel(
         def inverse_root(u):
             ci, t = units[u]
             c0, n = OUT_CHUNKS[ci]
+            if MODE[u] == "v":
+                both_sq = ring.tile([P, n], F32, name="both_sq")
+                nc.vector.scalar_tensor_tensor(
+                    both_sq[:], held[u]["sq"][:, 1, :], (0.625 * FETCH) ** 2, held[u]["sq"][:, 0, :], ALU.mult, ALU.add
+                )
+                root = ring.tile([P, n], F32, name="root")
+                nc.scalar.activation(root[:], both_sq[:], ACT.Abs_reciprocal_sqrt, bias=0.25, scale=0.5 / FETCH**2)
+                held[u]["root"] = root
+                return
             total = psum.tile([P, n], F32, name="total", tag="bank%d" % (u % 8))
             add_turned(total, held[u]["sq"][:, 0, :], held[u]["sq"][:, 1, :], n)
             root = ring.tile([P, n], F32, name="root")
@@ -253,13 +387,17 @@ def tile_picked_twtmxbstd_none_po_kernel(
             )
             nc.sync.dma_start(out=out_rows[:, t, cols], in_=results[ci][:, t, :])
             if t == PACK - 1:
-                o_woven = keep.tile([P, PACK * n], BF16, name="o_woven%d" % ci, align_bytes=64)
-                nc.vector.tensor_copy(*weave(o_woven[:], results[ci][:]))
-                nc.vector.quantize_mx(out=o_codes[:, cols].bitcast(FP8X4), scales=o_plane[:, cols], in_=o_woven[:])
+                parts = []
+                for k, w in pieces(ci, OUT_CHUNKS, OSUB):
+                    o_woven = keep.tile([P, PACK * w], BF16, name="o_woven%d_%d" % (ci, k), align_bytes=64)
+                    weave_on(OW_ENG[ci + k // w], o_woven[:], results[ci][:, :, k : k + w], w)
+                    parts.append((slice(c0 + k, c0 + k + w), o_woven))
+                for part, o_woven in parts:
+                    nc.vector.quantize_mx(out=o_codes[:, part].bitcast(FP8X4), scales=o_plane[:, part], in_=o_woven[:])
                 nc.sync.dma_start(out=o_words[:, cols], in_=o_codes[:, cols].bitcast(I32))
 
-        steps = ((fetch, 0), (both, 1), (finish, 3), (numerator, 1), (squares, 1), (inverse_root, 2))
-        for i in range(len(units) + 4):
+        steps = ((fetch, 0), (both, LAGS[0]), (finish, LAGS[1]), (numerator, LAGS[2]), (squares, LAGS[3]), (inverse_root, LAGS[4]))
+        for i in range(len(units) + max(LAGS)):
             for step, lag in steps:
                 if 0 <= i - lag < len(units):
                     step(i - lag)

@@ -23,30 +23,33 @@ HALF = 256
 MIX_CHUNKS = ((0,256,),(256,256,),)
 OUT_CHUNKS = ((0,256,),(256,256,),)
 FETCH = 0.6
-WARM = 0
+WARM = 1
 ORDER = "wb x n1 sl th n2 wa w1 gt w1s n3 n4"
 WB_ENG = "vv"
-EARLY = 1
-FB = 4
-MB = 5
+MG = 2
+OG = 2
+PG = 1
+FB = 3
+HW = 512
+MB = 4
 SUB = 0
-OSUB = 1
-MLAGS = (1,2,2,3,)
-PB_ENG = "vvvvvvvv"
+OSUB = 128
+MLAGS = (0,1,2,3,)
+PB_ENG = "vvvvvvssvvvv"
 W1_LATE = 0
 WB_SPLIT = 1
 WA_SPLIT = 2
 WA_ENG = "vv"
 D_ENG = "ssss"
-D2_ENG = "vvssssss"
-GT_ENG = "vvvvvvvv"
-ZW_ENG = "vvv"
-H_ENG = "ssssvsvs"
-PA_ENG = "ssssssss"
-MODE = "pppvppvp"
-OW_ENG = "vvs"
-W1_ENG = "s"
-LAGS = (1,6,4,2,4,)
+D2_ENG = "vvssssssssss"
+GT_ENG = "vvvvssvvvvvv"
+ZW_ENG = "vv"
+H_ENG = "ssssvsvsssss"
+PA_ENG = "ssssssssssss"
+MODE = "ppvvpppppppp"
+OW_ENG = "svs"
+W1_ENG = "v"
+LAGS = (0,4,3,1,3,)
 
 
 def weave(dst, src):
@@ -115,15 +118,24 @@ def tile_picked_twtmxbstd_none_po_kernel(
             else:
                 copy_on(eng, *weave(dst, src))
 
-        def gather_on(eng, dst, src, scale):
-            if eng == "s":
-                nc.scalar.activation(dst, src, ACT.Copy, scale=scale)
-            else:
-                nc.vector.tensor_scalar(dst, src, scale, 0.0, ALU.mult, ALU.add)
+        def gather_on(eng, dst, window, lst, c0, n, scale):
+            for k in range(0, n, HALF):
+                w = min(HALF, n - k)
+                src = window[:].indirect(entries(lst, c0 + k, w))
+                if eng == "s":
+                    nc.scalar.activation(dst[:, k : k + w], src, ACT.Copy, scale=scale)
+                else:
+                    nc.vector.tensor_scalar(dst[:, k : k + w], src, scale, 0.0, ALU.mult, ALU.add)
+
+        used = [PACK - 1]
+
+        def next_bank():
+            used.append((used[-1] + 1) % 8)
+            return "bank%d" % used[-1]
 
         xs = keep.tile([P, T], U8, name="xs", align_bytes=64)
         w1s_raw = keep.tile([P, N], U8, name="w1s_raw", align_bytes=64)
-        nc.vector.memset(w1s_raw[:].bitcast(I32), 0)
+        nc.gpsimd.memset(w1s_raw[:].bitcast(I32), 0)
         two_l = load_list(two, "two_l")
         for q in range(4):
             nc.sync.dma_start(
@@ -198,12 +210,16 @@ def tile_picked_twtmxbstd_none_po_kernel(
         offs_w = pick(xw, offs_l, U32, "offs_w")
 
         neg_b = keep.tile([P, PACK], F32, name="neg_b")
-        nc.vector.scalar_tensor_tensor(neg_b[:], sl_c[:], -1.0, th_c[:], ALU.mult, ALU.mult)
+        sl_th = keep.tile([P, PACK], F32, name="sl_th")
+        nc.gpsimd.tensor_tensor(sl_th[:], sl_c[:], th_c[:], ALU.mult)
+        nc.gpsimd.tensor_scalar(neg_b[:], sl_th[:], -1.0, 0.0, ALU.mult, ALU.add)
 
         wa_codes, wa_plane = quantise_weight(wa_raw, WA_ENG, "wa")
-        y_ps = [psum.tile([P, H], F32, name="y_ps%d" % t, tag="bank%d" % (PACK + t)) for t in range(PACK)]
-        for t in range(PACK):
-            product(y_ps[t][:], offs_w, offs_s, t, wa_codes[:], wa_plane[:])
+        y_ps = [psum.tile([P, 2, HALF], F32, name="y_ps%d" % b, tag="bank%d" % (PACK + b)) for b in range(PACK)]
+        for half in range(2):
+            cols = slice(half * HALF, (half + 1) * HALF)
+            for t in range(PACK):
+                product(y_ps[2 * half + t // 2][:, t % 2, :], offs_w, offs_s, t, wa_codes[:, cols], wa_plane[:, cols])
         w1w = keep.tile([P, N], U32, name="w1w", align_bytes=64)
         copy_on(W1_ENG, w1w[:].rearrange("p (t m) -> p t m", t=PACK), w1w_raw[:].rearrange("p (m t) -> p t m", t=PACK))
         w1s = keep.tile([P, N], U8, name="w1s", align_bytes=64)
@@ -213,58 +229,65 @@ def tile_picked_twtmxbstd_none_po_kernel(
 
         h_ps = []
         h_sb = [keep.tile([P, H], F32, name="h_sb%d" % t) for t in range(PACK)]
-        mix_units = [(ci, t) for ci in range(len(MIX_CHUNKS)) for t in range(PACK)]
-        z_rows = [keep.tile([P, PACK, n], BF16, name="z_rows%d" % ci) for ci, (c0, n) in enumerate(MIX_CHUNKS)]
+        mix_units = [(ci, t) for ci in range(2) for t in range(0, PACK, MG)]
+        z_rows = [keep.tile([P, PACK, HALF], BF16, name="z_rows%d" % ci) for ci in range(2)]
         mixed = {}
 
         def look_up(u):
-            ci, t = mix_units[u]
-            c0, n = MIX_CHUNKS[ci]
-            if ci == 0:
-                copy_on(D_ENG[t], d_sb[t][:], d_ps[t][:])
-            sg = ring.tile([P, n], F32, name="sg", bufs=MB)
-            nc.scalar.activation(
-                sg[:], d_sb[t][:].indirect(entries(n1_l, c0, n)), ACT.Sigmoid,
-                bias=neg_b[:, t : t + 1], scale=sl_c[:, t : t + 1],
-            )
-            d2 = ring.tile([P, n], F32, name="d2", bufs=MB)
-            gather_on(D2_ENG[u], d2[:], d_sb[t][:].indirect(entries(n2_l, c0, n)), 1.0)
+            ci, t0 = mix_units[u]
+            c0 = ci * HALF
+            sg = ring.tile([P, MG, HALF], F32, name="sg", bufs=MB)
+            d2 = ring.tile([P, MG, HALF], F32, name="d2", bufs=MB)
+            for g in range(MG):
+                t = t0 + g
+                if ci == 0:
+                    copy_on(D_ENG[t], d_sb[t][:], d_ps[t][:])
+                nc.scalar.activation(
+                    sg[:, g, :], d_sb[t][:].indirect(entries(n1_l, c0, HALF)), ACT.Sigmoid,
+                    bias=neg_b[:, t : t + 1], scale=sl_c[:, t : t + 1],
+                )
+                gather_on(D2_ENG[4 * ci + t], d2[:, g, :], d_sb[t], n2_l, c0, HALF, 1.0)
             if WARM and u == len(mix_units) - 1:
-                nc.scalar.activation(warm[:, 1:2], sg[:, 0:1], ACT.Abs_reciprocal_sqrt, bias=0.25)
+                nc.scalar.activation(warm[:, 1:2], sg[:, MG - 1, 0:1], ACT.Abs_reciprocal_sqrt, bias=0.25)
             mixed[u] = dict(sg=sg, d2=d2)
 
         def candidates(u):
-            ci, t = mix_units[u]
-            c0, n = MIX_CHUNKS[ci]
-            diff = ring.tile([P, n], F32, name="diff")
-            nc.vector.tensor_tensor(diff[:], mixed[u]["d2"][:], d_sb[t][:, c0 : c0 + n], ALU.subtract)
-            gated = ring.tile([P, n], F32, name="gated")
-            nc.vector.tensor_tensor(gated[:], y_ps[t][:, c0 : c0 + n], mixed[u]["sg"][:], ALU.mult)
+            ci, t0 = mix_units[u]
+            c0 = ci * HALF
+            diff = ring.tile([P, MG, HALF], F32, name="diff")
+            for g in range(MG):
+                nc.vector.tensor_tensor(
+                    diff[:, g, :], mixed[u]["d2"][:, g, :], d_sb[t0 + g][:, c0 : c0 + HALF], ALU.subtract
+                )
+            gated = ring.tile([P, MG, HALF], F32, name="gated")
+            y_part = y_ps[2 * ci + t0 // 2][:, t0 % 2 : t0 % 2 + MG, :]
+            nc.vector.tensor_tensor(gated[:], y_part, mixed[u]["sg"][:], ALU.mult)
             mixed[u]["diff"], mixed[u]["gated"] = diff, gated
 
         def larger(u):
-            ci, t = mix_units[u]
-            big = ring.tile([P, MIX_CHUNKS[ci][1]], F32, name="big")
+            big = ring.tile([P, MG, HALF], F32, name="big")
             nc.vector.tensor_tensor(big[:], mixed[u]["gated"][:], mixed[u]["diff"][:], ALU.max)
             mixed[u]["big"] = big
 
         def weigh(u):
-            ci, t = mix_units[u]
-            if GT_ENG[u] == "v":
-                nc.vector.tensor_scalar_mul(z_rows[ci][:, t, :], mixed[u]["big"][:], gt_c[:, t : t + 1])
-            else:
-                nc.scalar.activation(z_rows[ci][:, t, :], mixed[u]["big"][:], ACT.Copy, scale=gt_c[:, t : t + 1])
+            ci, t0 = mix_units[u]
+            for g in range(MG):
+                t = t0 + g
+                if GT_ENG[4 * ci + t] == "v":
+                    nc.vector.tensor_scalar_mul(z_rows[ci][:, t, :], mixed[u]["big"][:, g, :], gt_c[:, t : t + 1])
+                else:
+                    nc.scalar.activation(z_rows[ci][:, t, :], mixed[u]["big"][:, g, :], ACT.Copy, scale=gt_c[:, t : t + 1])
 
         woven_z = {}
 
         def pieces(ci, chunks, sub):
             c0, n = chunks[ci]
-            w = P if (sub and ci == len(chunks) - 1) else n
+            w = sub if (sub and ci == len(chunks) - 1) else n
             return [(k, w) for k in range(0, n, w)]
 
         def weave_z(u):
             ci, t = mix_units[u]
-            if t == PACK - 1:
+            if t == PACK - MG:
                 for k, w in pieces(ci, MIX_CHUNKS, SUB):
                     zw = keep.tile([P, PACK * w], BF16, name="z_woven%d_%d" % (ci, k), align_bytes=64)
                     weave_on(ZW_ENG[ci + k // w], zw[:], z_rows[ci][:, :, k : k + w], w)
@@ -272,7 +295,7 @@ def tile_picked_twtmxbstd_none_po_kernel(
 
         def mix_product(u):
             ci, t = mix_units[u]
-            if t == PACK - 1:
+            if t == PACK - MG:
                 if ci == 0:
                     for j in range(PACK):
                         h_ps.append(psum.tile([P, H], F32, name="h_ps%d" % j, tag="bank%d" % j))
@@ -283,8 +306,11 @@ def tile_picked_twtmxbstd_none_po_kernel(
                     nc.vector.quantize_mx(out=z_codes[:].bitcast(FP8X4), scales=z_plane[:], in_=woven_z[ci, k][:])
                     for j in range(PACK):
                         product(h_ps[j][:, c0 + k : c0 + k + w], w1w, w1s, j, z_codes[:], z_plane[:])
-                for j in range(PACK):
-                    copy_on(H_ENG[4 * ci + j], h_sb[j][:, c0 : c0 + n], h_ps[j][:, c0 : c0 + n])
+                hw = min(n, HW)
+                for k in range(0, n, hw):
+                    for j in range(PACK):
+                        cols = slice(c0 + k, c0 + k + hw)
+                        copy_on(H_ENG[4 * (ci + k // hw) + j], h_sb[j][:, cols], h_ps[j][:, cols])
 
         steps = ((look_up, 0), (candidates, 0), (mix_product, MLAGS[3]), (larger, MLAGS[0]), (weigh, MLAGS[1]), (weave_z, MLAGS[2]))
         for i in range(len(mix_units) + max(MLAGS)):
@@ -297,96 +323,102 @@ def tile_picked_twtmxbstd_none_po_kernel(
         o_plane = keep.tile([P, H], U8, name="o_plane", align_bytes=64)
         o_words = out_1[0].rearrange("p n t -> p (n t)").bitcast(I32)
         results = [keep.tile([P, PACK, n], F32, name="result%d" % ci) for ci, (c0, n) in enumerate(OUT_CHUNKS)]
-        units = [(ci, t) for ci in range(len(OUT_CHUNKS)) for t in range(PACK)]
+        units = [(ci, t) for ci in range(len(OUT_CHUNKS)) for t in range(0, PACK, OG)]
         held = {}
 
-        def add_turned(bank, first, second, n):
-            for b in range(n // P):
-                blk = slice(b * P, (b + 1) * P)
-                nc.tensor.matmul(bank[:, blk], first[:, blk], ident[:], start=True, stop=False, is_transpose=True)
-                nc.tensor.matmul(bank[:, blk], second[:, blk], ident[:], start=False, stop=True, is_transpose=True)
-
         def fetch(u):
-            ci, t = units[u]
+            ci, t0 = units[u]
             c0, n = OUT_CHUNKS[ci]
-            pa = ring.tile([P, n], F32, name="pa", bufs=FB)
-            gather_on(PA_ENG[u], pa[:], h_sb[t][:].indirect(entries(n3_l, c0, n)), FETCH)
-            pb = ring.tile([P, n], F32, name="pb", bufs=FB)
-            gather_on(PB_ENG[u], pb[:], h_sb[t][:].indirect(entries(n4_l, c0, n)), -FETCH)
+            pa = ring.tile([P, OG, n], F32, name="pa", bufs=FB)
+            pb = ring.tile([P, OG, n], F32, name="pb", bufs=FB)
+            for g in range(OG):
+                t = t0 + g
+                gather_on(PA_ENG[4 * ci + t], pa[:, g, :], h_sb[t], n3_l, c0, n, FETCH)
+                gather_on(PB_ENG[4 * ci + t], pb[:, g, :], h_sb[t], n4_l, c0, n, -FETCH)
             held[u] = dict(pa=pa, pb=pb)
 
         def both(u):
-            ci, t = units[u]
+            ci, t0 = units[u]
             c0, n = OUT_CHUNKS[ci]
-            pair = ring.tile([P, n], F32, name="pair")
-            nc.vector.tensor_tensor(pair[:], held[u]["pb"][:], held[u]["pa"][:], ALU.subtract)
+            pair = ring.tile([P, OG, n], F32, name="pair", bufs=6)
+            if PG:
+                nc.vector.tensor_tensor(pair[:], held[u]["pb"][:], held[u]["pa"][:], ALU.subtract)
+            else:
+                for g in range(OG):
+                    nc.vector.tensor_tensor(pair[:, g, :], held[u]["pb"][:, g, :], held[u]["pa"][:, g, :], ALU.subtract)
             held[u]["pair"] = pair
 
         def numerator(u):
-            ci, t = units[u]
+            ci, t0 = units[u]
             c0, n = OUT_CHUNKS[ci]
-            num = ring.tile([P, n], F32, name="num", bufs=6)
-            nc.vector.scalar_tensor_tensor(
-                num[:], held[u]["pair"][:], 5.0 / 11.0 / FETCH, h_sb[t][:, c0 : c0 + n], ALU.mult, ALU.add
-            )
+            num = ring.tile([P, OG, n], F32, name="num", bufs=6)
+            for g in range(OG):
+                nc.vector.scalar_tensor_tensor(
+                    num[:, g, :], held[u]["pair"][:, g, :], 5.0 / 11.0 / FETCH, h_sb[t0 + g][:, c0 : c0 + n],
+                    ALU.mult, ALU.add,
+                )
             held[u]["num"] = num
 
         def squares(u):
-            ci, t = units[u]
+            ci, t0 = units[u]
             c0, n = OUT_CHUNKS[ci]
-            if MODE[u] == "v":
-                forms = ring.tile([P, 2, n], F32, name="forms")
-                nc.vector.tensor_tensor(forms[:, 0, :], held[u]["pa"][:], held[u]["pb"][:], ALU.add)
-                nc.vector.tensor_tensor(forms[:, 1, :], h_sb[t][:, c0 : c0 + n], held[u]["pair"][:], ALU.add)
-                sq = ring.tile([P, 2, n], F32, name="sq")
-                nc.scalar.activation(sq[:], forms[:], ACT.Square)
-                held[u]["sq"] = sq
-                return
-            turned = psum.tile([P, 2, n], F32, name="turned", tag="bank%d" % ((PACK + u) % 8))
-            if EARLY:
-                terms = ((1, h_sb[t][:, c0 : c0 + n]), (0, held[u]["pa"]), (0, held[u]["pb"]), (1, held[u]["pair"]))
-                passes = [(half, src, b) for half, src in terms for b in range(n // P)]
-                for k, (half, src, b) in enumerate(passes):
-                    blk = slice(b * P, (b + 1) * P)
-                    nc.tensor.matmul(
-                        turned[:, half, blk], src[:, blk], ident[:],
-                        start=(k == 0), stop=(k == len(passes) - 1), is_transpose=True,
-                    )
-            else:
-                add_turned(turned[:, 0, :], held[u]["pa"], held[u]["pb"], n)
-                add_turned(turned[:, 1, :], h_sb[t][:, c0 : c0 + n], held[u]["pair"], n)
-            sq = ring.tile([P, 2, n], F32, name="sq")
-            nc.scalar.activation(sq[:, 0, :], turned[:, 0, :], ACT.Square, scale=math.sqrt(0.5) / FETCH)
-            nc.scalar.activation(sq[:, 1, :], turned[:, 1, :], ACT.Square, scale=math.sqrt(0.5) * 0.625)
+            sq = ring.tile([P, OG, 2, n], F32, name="sq")
             held[u]["sq"] = sq
+            for g in range(OG):
+                h_part = h_sb[t0 + g][:, c0 : c0 + n]
+                pa, pb, pair = held[u]["pa"][:, g, :], held[u]["pb"][:, g, :], held[u]["pair"][:, g, :]
+                if MODE[4 * ci + t0] == "v":
+                    forms = ring.tile([P, 2, n], F32, name="forms")
+                    nc.vector.tensor_tensor(forms[:, 0, :], pa, pb, ALU.add)
+                    nc.vector.tensor_tensor(forms[:, 1, :], h_part, pair, ALU.add)
+                    nc.scalar.activation(sq[:, g, :, :], forms[:], ACT.Square)
+                else:
+                    turned = psum.tile([P, 2, n], F32, name="turned", tag=next_bank())
+                    terms = ((1, h_part), (0, pa), (0, pb), (1, pair))
+                    passes = [(half, src, b) for half, src in terms for b in range(n // P)]
+                    for k, (half, src, b) in enumerate(passes):
+                        blk = slice(b * P, (b + 1) * P)
+                        nc.tensor.matmul(
+                            turned[:, half, blk], src[:, blk], ident[:],
+                            start=(k == 0), stop=(k == len(passes) - 1), is_transpose=True,
+                        )
+                    nc.scalar.activation(sq[:, g, 0, :], turned[:, 0, :], ACT.Square, scale=math.sqrt(0.5) / FETCH)
+                    nc.scalar.activation(sq[:, g, 1, :], turned[:, 1, :], ACT.Square, scale=math.sqrt(0.5) * 0.625)
 
         def inverse_root(u):
-            ci, t = units[u]
+            ci, t0 = units[u]
             c0, n = OUT_CHUNKS[ci]
-            if MODE[u] == "v":
-                both_sq = ring.tile([P, n], F32, name="both_sq")
-                nc.vector.scalar_tensor_tensor(
-                    both_sq[:], held[u]["sq"][:, 1, :], (0.625 * FETCH) ** 2, held[u]["sq"][:, 0, :], ALU.mult, ALU.add
-                )
-                root = ring.tile([P, n], F32, name="root")
-                nc.scalar.activation(root[:], both_sq[:], ACT.Abs_reciprocal_sqrt, bias=0.25, scale=0.5 / FETCH**2)
-                held[u]["root"] = root
-                return
-            total = psum.tile([P, n], F32, name="total", tag="bank%d" % (u % 8))
-            add_turned(total, held[u]["sq"][:, 0, :], held[u]["sq"][:, 1, :], n)
-            root = ring.tile([P, n], F32, name="root")
-            nc.scalar.activation(root[:], total[:], ACT.Abs_reciprocal_sqrt, bias=0.25)
+            sq = held[u]["sq"]
+            root = ring.tile([P, OG, n], F32, name="root")
             held[u]["root"] = root
+            if MODE[4 * ci + t0] == "v":
+                both_sq = ring.tile([P, OG, n], F32, name="both_sq")
+                nc.vector.scalar_tensor_tensor(
+                    both_sq[:], sq[:, :, 1, :], (0.625 * FETCH) ** 2, sq[:, :, 0, :], ALU.mult, ALU.add
+                )
+                nc.scalar.activation(root[:], both_sq[:], ACT.Abs_reciprocal_sqrt, bias=0.25, scale=0.5 / FETCH**2)
+            else:
+                total = psum.tile([P, OG, n], F32, name="total", tag=next_bank())
+                for g in range(OG):
+                    for b in range(n // P):
+                        blk = slice(b * P, (b + 1) * P)
+                        for k in range(2):
+                            nc.tensor.matmul(
+                                total[:, g, blk], sq[:, g, k, blk], ident[:],
+                                start=(k == 0), stop=(k == 1), is_transpose=True,
+                            )
+                nc.scalar.activation(root[:], total[:], ACT.Abs_reciprocal_sqrt, bias=0.25)
 
         def finish(u):
-            ci, t = units[u]
+            ci, t0 = units[u]
             c0, n = OUT_CHUNKS[ci]
             cols = slice(c0, c0 + n)
+            rows = slice(t0, t0 + OG)
             nc.vector.scalar_tensor_tensor(
-                results[ci][:, t, :], held[u]["num"][:], 0.6875, held[u]["root"][:], ALU.mult, ALU.mult
+                results[ci][:, rows, :], held[u]["num"][:], 0.6875, held[u]["root"][:], ALU.mult, ALU.mult
             )
-            nc.sync.dma_start(out=out_rows[:, t, cols], in_=results[ci][:, t, :])
-            if t == PACK - 1:
+            nc.sync.dma_start(out=out_rows[:, rows, cols], in_=results[ci][:, rows, :])
+            if t0 == PACK - OG:
                 parts = []
                 for k, w in pieces(ci, OUT_CHUNKS, OSUB):
                     o_woven = keep.tile([P, PACK * w], BF16, name="o_woven%d_%d" % (ci, k), align_bytes=64)

@@ -4,7 +4,7 @@ from contextlib import ExitStack
 import concourse.mybir as mybir
 from concourse.masks import make_identity
 
-K, T, S, H, N = 512, 2048, 512, 512, 512
+T, S, H, N = 2048, 512, 512, 512
 FLOPS = 3 * 2 * 512 * 512 * 512
 
 F32 = mybir.dt.float32
@@ -20,36 +20,15 @@ ACT = mybir.ActivationFunctionType
 P = 128
 PACK = 4
 HALF = 256
-MIX_CHUNKS = ((0,256,),(256,256,),)
-OUT_CHUNKS = ((0,256,),(256,256,),)
+PAIR = 2
+BANKS = 8
+GROUPS = [(half, t0) for half in range(2) for t0 in range(0, PACK, PAIR)]
+
+N2_ON_VECTOR = 3
+WEIGH_ON_SCALAR = 2
+SUMS_ON_VECTOR = 1
+
 FETCH = 0.6
-WARM = 1
-ORDER = "wb x n1 sl th n2 wa w1 gt w1s n3 n4"
-WB_ENG = "vv"
-MG = 2
-OG = 2
-PG = 1
-FB = 3
-HW = 512
-MB = 4
-SUB = 0
-OSUB = 128
-MLAGS = (0,1,2,3,)
-PB_ENG = "vvvvvvssvvvv"
-W1_LATE = 0
-WB_SPLIT = 1
-WA_SPLIT = 2
-WA_ENG = "vv"
-D_ENG = "ssss"
-D2_ENG = "vvssssssssss"
-GT_ENG = "vvvvssvvvvvv"
-ZW_ENG = "vv"
-H_ENG = "ssssvsvsssss"
-PA_ENG = "ssssssssssss"
-MODE = "ppvvpppppppp"
-OW_ENG = "svs"
-W1_ENG = "v"
-LAGS = (0,4,3,1,3,)
 
 
 def weave(dst, src):
@@ -59,8 +38,23 @@ def weave(dst, src):
     )
 
 
-def entries(lst, c0, n):
-    return lst[:, c0 // 16 : (c0 + n) // 16]
+def deal(dst, src):
+    return dst.rearrange("p (t m) -> p t m", t=PACK), src.rearrange("p (m t) -> p t m", t=PACK)
+
+
+def half_columns(half):
+    return slice(half * HALF, (half + 1) * HALF)
+
+
+def half_entries(lst, half):
+    return lst[:, half * HALF // 16 : (half + 1) * HALF // 16]
+
+
+def pipeline(steps):
+    for i in range(len(GROUPS) + max(lag for step, lag in steps)):
+        for step, lag in steps:
+            if 0 <= i - lag < len(GROUPS):
+                step(i - lag)
 
 
 def tile_picked_twtmxbstd_none_po_kernel(
@@ -69,7 +63,7 @@ def tile_picked_twtmxbstd_none_po_kernel(
     nc = tc.nc
     with ExitStack() as ctx:
         keep = ctx.enter_context(tc.tile_pool(name="keep", bufs=1))
-        ring = ctx.enter_context(tc.tile_pool(name="ring", bufs=4))
+        per_group = ctx.enter_context(tc.tile_pool(name="per_group", bufs=len(GROUPS)))
         psum = ctx.enter_context(tc.psum_pool(name="psum", bufs=1))
 
         def load_list(src, name):
@@ -77,120 +71,69 @@ def tile_picked_twtmxbstd_none_po_kernel(
             nc.sync.dma_start(lst[:], src)
             return lst
 
-        def load_scale_rows(plane, src):
-            for q in range(4):
-                nc.sync.dma_start(
-                    out=plane[32 * q : 32 * q + 4, :].bitcast(I32),
-                    in_=src[0, 4 * q : 4 * q + 4, :].bitcast(I32),
-                )
+        def load_words(src, width, name):
+            words = keep.tile([P, width], U32, name=name, align_bytes=64)
+            nc.sync.dma_start(out=words[:].bitcast(I32), in_=src[0].rearrange("p n t -> p (n t)").bitcast(I32))
+            return words
 
         def load_column(src, name):
             col = keep.tile([P, PACK], F32, name=name)
             nc.sync.dma_start(out=col[:], in_=src.rearrange("(p t) o -> p (t o)", t=PACK))
             return col
 
-        def load_weight(w, split, name):
-            view = w.rearrange("(p j) c -> p j c", j=PACK)
-            if split == 1:
-                raw = keep.tile([P, PACK, H], F32, name=name)
-                nc.sync.dma_start(out=raw[:], in_=view)
-                return [raw[:, :, :HALF], raw[:, :, HALF:]]
-            raws = []
-            for half in range(2):
-                raw = keep.tile([P, PACK, HALF], F32, name=name + str(half))
-                nc.sync.dma_start(out=raw[:], in_=view[:, :, half * HALF : (half + 1) * HALF])
-                raws.append(raw[:])
-            return raws
+        def load_weight(w, cols, name):
+            raw = keep.tile([P, PACK, cols.stop - cols.start], F32, name=name)
+            nc.sync.dma_start(out=raw[:], in_=w.rearrange("(p j) c -> p j c", j=PACK)[:, :, cols])
+            return raw
 
-        def copy_on(eng, dst, src):
-            if eng == "s":
-                nc.scalar.copy(dst, src)
-            else:
-                nc.vector.tensor_copy(dst, src)
-
-        def weave_on(eng, dst, src, n):
-            if eng == "b":
-                nc.scalar.copy(*weave(dst[:, : n], src[:, :, : n // 4]))
-                nc.vector.tensor_copy(*weave(dst[:, n :], src[:, :, n // 4 :]))
-            elif eng == "h":
-                nc.scalar.copy(*weave(dst[:, : 2 * n], src[:, :, : n // 2]))
-                nc.vector.tensor_copy(*weave(dst[:, 2 * n :], src[:, :, n // 2 :]))
-            else:
-                copy_on(eng, *weave(dst, src))
-
-        def gather_on(eng, dst, window, lst, c0, n, scale):
-            for k in range(0, n, HALF):
-                w = min(HALF, n - k)
-                src = window[:].indirect(entries(lst, c0 + k, w))
-                if eng == "s":
-                    nc.scalar.activation(dst[:, k : k + w], src, ACT.Copy, scale=scale)
-                else:
-                    nc.vector.tensor_scalar(dst[:, k : k + w], src, scale, 0.0, ALU.mult, ALU.add)
-
-        used = [PACK - 1]
-
-        def next_bank():
-            used.append((used[-1] + 1) % 8)
-            return "bank%d" % used[-1]
-
-        xs = keep.tile([P, T], U8, name="xs", align_bytes=64)
-        w1s_raw = keep.tile([P, N], U8, name="w1s_raw", align_bytes=64)
-        nc.gpsimd.memset(w1s_raw[:].bitcast(I32), 0)
+        x_plane = keep.tile([P, T], U8, name="x_plane", align_bytes=64)
+        w1_plane_raw = keep.tile([P, N], U8, name="w1_plane_raw", align_bytes=64)
+        nc.gpsimd.memset(w1_plane_raw[:].bitcast(I32), 0)
         two_l = load_list(two, "two_l")
         for q in range(4):
             nc.sync.dma_start(
-                out=xs[32 * q : 32 * q + 32, :].bitcast(I32),
+                out=x_plane[32 * q : 32 * q + 32, :].bitcast(I32),
                 in_=x_scales[0, 4 * q : 4 * q + 4, :].bitcast(I32).partition_broadcast(8),
             )
         offs_l = load_list(offs, "offs_l")
-        got = {}
-
-        def load_words(src, width, name):
-            words = keep.tile([P, width], U32, name=name, align_bytes=64)
-            nc.sync.dma_start(out=words[:].bitcast(I32), in_=src[0].rearrange("p n t -> p (n t)").bitcast(I32))
-            return words
-
-        for key in ORDER.split():
-            if key == "x":
-                xw = load_words(x_words, T, "xw")
-            elif key == "wb":
-                wb_raw = load_weight(wb, WB_SPLIT, "wb_raw")
-            elif key == "wa":
-                wa_raw = load_weight(wa, WA_SPLIT, "wa_raw")
-            elif key == "w1":
-                w1w_raw = load_words(w1_words, N, "w1w_raw")
-            elif key == "w1s":
-                load_scale_rows(w1s_raw, w1_scales)
-            elif key in ("sl", "th", "gt"):
-                got[key] = load_column(dict(sl=sl, th=th, gt=gt)[key], key + "_c")
-            else:
-                got[key] = load_list(dict(n1=n1, n2=n2, n3=n3, n4=n4)[key], key + "_l")
-        sl_c, th_c, gt_c = got["sl"], got["th"], got["gt"]
-        n1_l, n2_l, n3_l, n4_l = got["n1"], got["n2"], got["n3"], got["n4"]
+        wb_raw = load_weight(wb, slice(0, H), "wb_raw")
+        x_codes = load_words(x_words, T, "x_codes")
+        n1_l = load_list(n1, "n1_l")
+        sl_c = load_column(sl, "sl_c")
+        th_c = load_column(th, "th_c")
+        n2_l = load_list(n2, "n2_l")
+        wa_raw = [load_weight(wa, half_columns(half), "wa_raw%d" % half) for half in range(2)]
+        w1_codes_raw = load_words(w1_words, N, "w1_codes_raw")
+        gt_c = load_column(gt, "gt_c")
+        for q in range(4):
+            nc.sync.dma_start(
+                out=w1_plane_raw[32 * q : 32 * q + 4, :].bitcast(I32),
+                in_=w1_scales[0, 4 * q : 4 * q + 4, :].bitcast(I32),
+            )
+        n3_l = load_list(n3, "n3_l")
+        n4_l = load_list(n4, "n4_l")
         ident = keep.tile([P, P], F32, name="ident")
         make_identity(nc, ident[:])
-        if WARM:
-            warm = keep.tile([P, 2], F32, name="warm")
 
         def pick(window, lst, dtype, name):
-            got = keep.tile([P, S], dtype, name=name, align_bytes=64)
-            nc.vector.tensor_copy(got[:].rearrange("p (t m) -> p m t", t=PACK), window[:].indirect(lst[:]))
-            return got
+            picked = keep.tile([P, S], dtype, name=name, align_bytes=64)
+            nc.vector.tensor_copy(picked[:].rearrange("p (t m) -> p m t", t=PACK), window[:].indirect(lst[:]))
+            return picked
 
-        def quantise_weight(raws, engs, name):
+        def quantise_weight(halves, name):
             codes = keep.tile([P, H], U32, name=name + "_codes", align_bytes=64)
             plane = keep.tile([P, H], U8, name=name + "_plane", align_bytes=64)
             for half in range(2):
                 woven = keep.tile([P, PACK * HALF], BF16, name=name + "_woven%d" % half, align_bytes=64)
-                weave_on(engs[half], woven[:], raws[half], HALF)
-                cols = slice(half * HALF, (half + 1) * HALF)
+                nc.vector.tensor_copy(*weave(woven[:], halves[half]))
+                cols = half_columns(half)
                 nc.vector.quantize_mx(out=codes[:, cols].bitcast(FP8X4), scales=plane[:, cols], in_=woven[:])
             return codes, plane
 
-        def product(bank, lhs_codes, lhs_plane, t, rhs_codes, rhs_plane):
+        def product(result, lhs_codes, lhs_plane, t, rhs_codes, rhs_plane):
             cols = slice(t * P, (t + 1) * P)
             nc.tensor.matmul_mx(
-                out=bank,
+                out=result,
                 lhsT=lhs_codes[:, cols].bitcast(FP8X4),
                 lhsT_scale=lhs_plane[:, cols],
                 rhs=rhs_codes.bitcast(FP8X4),
@@ -199,242 +142,219 @@ def tile_picked_twtmxbstd_none_po_kernel(
                 stop=True,
             )
 
-        two_s = pick(xs, two_l, U8, "two_s")
-        offs_s = pick(xs, offs_l, U8, "offs_s")
-        wb_codes, wb_plane = quantise_weight(wb_raw, WB_ENG, "wb")
-        two_w = pick(xw, two_l, U32, "two_w")
+        two_plane = pick(x_plane, two_l, U8, "two_plane")
+        offs_plane = pick(x_plane, offs_l, U8, "offs_plane")
+        wb_codes, wb_plane = quantise_weight([wb_raw[:, :, half_columns(half)] for half in range(2)], "wb")
+        two_codes = pick(x_codes, two_l, U32, "two_codes")
         d_ps = [psum.tile([P, H], F32, name="d_ps%d" % t, tag="bank%d" % t) for t in range(PACK)]
         d_sb = [keep.tile([P, H], F32, name="d_sb%d" % t) for t in range(PACK)]
         for t in range(PACK):
-            product(d_ps[t][:], two_w, two_s, t, wb_codes[:], wb_plane[:])
-        offs_w = pick(xw, offs_l, U32, "offs_w")
+            product(d_ps[t][:], two_codes, two_plane, t, wb_codes[:], wb_plane[:])
+        offs_codes = pick(x_codes, offs_l, U32, "offs_codes")
 
-        neg_b = keep.tile([P, PACK], F32, name="neg_b")
         sl_th = keep.tile([P, PACK], F32, name="sl_th")
+        sg_bias = keep.tile([P, PACK], F32, name="sg_bias")
         nc.gpsimd.tensor_tensor(sl_th[:], sl_c[:], th_c[:], ALU.mult)
-        nc.gpsimd.tensor_scalar(neg_b[:], sl_th[:], -1.0, 0.0, ALU.mult, ALU.add)
+        nc.gpsimd.tensor_scalar(sg_bias[:], sl_th[:], -1.0, 0.0, ALU.mult, ALU.add)
 
-        wa_codes, wa_plane = quantise_weight(wa_raw, WA_ENG, "wa")
-        y_ps = [psum.tile([P, 2, HALF], F32, name="y_ps%d" % b, tag="bank%d" % (PACK + b)) for b in range(PACK)]
-        for half in range(2):
-            cols = slice(half * HALF, (half + 1) * HALF)
-            for t in range(PACK):
-                product(y_ps[2 * half + t // 2][:, t % 2, :], offs_w, offs_s, t, wa_codes[:, cols], wa_plane[:, cols])
-        w1w = keep.tile([P, N], U32, name="w1w", align_bytes=64)
-        copy_on(W1_ENG, w1w[:].rearrange("p (t m) -> p t m", t=PACK), w1w_raw[:].rearrange("p (m t) -> p t m", t=PACK))
-        w1s = keep.tile([P, N], U8, name="w1s", align_bytes=64)
-        nc.vector.tensor_copy(
-            w1s[:].rearrange("p (t m) -> p t m", t=PACK), w1s_raw[:].rearrange("p (m t) -> p t m", t=PACK)
-        )
+        wa_codes, wa_plane = quantise_weight([raw[:] for raw in wa_raw], "wa")
+        y_ps = [psum.tile([P, PAIR, HALF], F32, name="y_ps%d" % g, tag="bank%d" % (PACK + g)) for g in range(len(GROUPS))]
+        for g, (half, t0) in enumerate(GROUPS):
+            cols = half_columns(half)
+            for k in range(PAIR):
+                product(y_ps[g][:, k, :], offs_codes, offs_plane, t0 + k, wa_codes[:, cols], wa_plane[:, cols])
+
+        w1_codes = keep.tile([P, N], U32, name="w1_codes", align_bytes=64)
+        nc.vector.tensor_copy(*deal(w1_codes[:], w1_codes_raw[:]))
+        w1_plane = keep.tile([P, N], U8, name="w1_plane", align_bytes=64)
+        nc.vector.tensor_copy(*deal(w1_plane[:], w1_plane_raw[:]))
 
         h_ps = []
         h_sb = [keep.tile([P, H], F32, name="h_sb%d" % t) for t in range(PACK)]
-        mix_units = [(ci, t) for ci in range(2) for t in range(0, PACK, MG)]
-        z_rows = [keep.tile([P, PACK, HALF], BF16, name="z_rows%d" % ci) for ci in range(2)]
-        mixed = {}
+        z_rows = [keep.tile([P, PACK, HALF], BF16, name="z_rows%d" % half) for half in range(2)]
+        z_woven = [keep.tile([P, PACK * HALF], BF16, name="z_woven%d" % half, align_bytes=64) for half in range(2)]
+        mix = [dict() for g in GROUPS]
 
-        def look_up(u):
-            ci, t0 = mix_units[u]
-            c0 = ci * HALF
-            sg = ring.tile([P, MG, HALF], F32, name="sg", bufs=MB)
-            d2 = ring.tile([P, MG, HALF], F32, name="d2", bufs=MB)
-            for g in range(MG):
-                t = t0 + g
-                if ci == 0:
-                    copy_on(D_ENG[t], d_sb[t][:], d_ps[t][:])
+        def group_tile(name):
+            return per_group.tile([P, PAIR, HALF], F32, name=name)
+
+        def look_up_d(g):
+            half, t0 = GROUPS[g]
+            sg, d2 = group_tile("sg"), group_tile("d2")
+            for k in range(PAIR):
+                t = t0 + k
+                if half == 0:
+                    nc.scalar.copy(d_sb[t][:], d_ps[t][:])
                 nc.scalar.activation(
-                    sg[:, g, :], d_sb[t][:].indirect(entries(n1_l, c0, HALF)), ACT.Sigmoid,
-                    bias=neg_b[:, t : t + 1], scale=sl_c[:, t : t + 1],
+                    sg[:, k, :], d_sb[t][:].indirect(half_entries(n1_l, half)), ACT.Sigmoid,
+                    bias=sg_bias[:, t : t + 1], scale=sl_c[:, t : t + 1],
                 )
-                gather_on(D2_ENG[4 * ci + t], d2[:, g, :], d_sb[t], n2_l, c0, HALF, 1.0)
-            if WARM and u == len(mix_units) - 1:
-                nc.scalar.activation(warm[:, 1:2], sg[:, MG - 1, 0:1], ACT.Abs_reciprocal_sqrt, bias=0.25)
-            mixed[u] = dict(sg=sg, d2=d2)
-
-        def candidates(u):
-            ci, t0 = mix_units[u]
-            c0 = ci * HALF
-            diff = ring.tile([P, MG, HALF], F32, name="diff")
-            for g in range(MG):
-                nc.vector.tensor_tensor(
-                    diff[:, g, :], mixed[u]["d2"][:, g, :], d_sb[t0 + g][:, c0 : c0 + HALF], ALU.subtract
-                )
-            gated = ring.tile([P, MG, HALF], F32, name="gated")
-            y_part = y_ps[2 * ci + t0 // 2][:, t0 % 2 : t0 % 2 + MG, :]
-            nc.vector.tensor_tensor(gated[:], y_part, mixed[u]["sg"][:], ALU.mult)
-            mixed[u]["diff"], mixed[u]["gated"] = diff, gated
-
-        def larger(u):
-            big = ring.tile([P, MG, HALF], F32, name="big")
-            nc.vector.tensor_tensor(big[:], mixed[u]["gated"][:], mixed[u]["diff"][:], ALU.max)
-            mixed[u]["big"] = big
-
-        def weigh(u):
-            ci, t0 = mix_units[u]
-            for g in range(MG):
-                t = t0 + g
-                if GT_ENG[4 * ci + t] == "v":
-                    nc.vector.tensor_scalar_mul(z_rows[ci][:, t, :], mixed[u]["big"][:, g, :], gt_c[:, t : t + 1])
+                by_n2 = d_sb[t][:].indirect(half_entries(n2_l, half))
+                if PAIR * g + k < N2_ON_VECTOR:
+                    nc.vector.tensor_copy(d2[:, k, :], by_n2)
                 else:
-                    nc.scalar.activation(z_rows[ci][:, t, :], mixed[u]["big"][:, g, :], ACT.Copy, scale=gt_c[:, t : t + 1])
+                    nc.scalar.activation(d2[:, k, :], by_n2, ACT.Copy)
+            if g == len(GROUPS) - 1:
+                warm = keep.tile([P, 1], F32, name="warm")
+                nc.scalar.activation(warm[:], sg[:, PAIR - 1, 0:1], ACT.Abs_reciprocal_sqrt, bias=0.25)
+            mix[g]["sg"], mix[g]["d2"] = sg, d2
 
-        woven_z = {}
+        def candidates(g):
+            half, t0 = GROUPS[g]
+            diff, gated = group_tile("diff"), group_tile("gated")
+            for k in range(PAIR):
+                own = d_sb[t0 + k][:, half_columns(half)]
+                nc.vector.tensor_tensor(diff[:, k, :], mix[g]["d2"][:, k, :], own, ALU.subtract)
+            nc.vector.tensor_tensor(gated[:], y_ps[g][:], mix[g]["sg"][:], ALU.mult)
+            mix[g]["diff"], mix[g]["gated"] = diff, gated
 
-        def pieces(ci, chunks, sub):
-            c0, n = chunks[ci]
-            w = sub if (sub and ci == len(chunks) - 1) else n
-            return [(k, w) for k in range(0, n, w)]
+        def larger(g):
+            big = group_tile("big")
+            nc.vector.tensor_tensor(big[:], mix[g]["gated"][:], mix[g]["diff"][:], ALU.max)
+            mix[g]["big"] = big
 
-        def weave_z(u):
-            ci, t = mix_units[u]
-            if t == PACK - MG:
-                for k, w in pieces(ci, MIX_CHUNKS, SUB):
-                    zw = keep.tile([P, PACK * w], BF16, name="z_woven%d_%d" % (ci, k), align_bytes=64)
-                    weave_on(ZW_ENG[ci + k // w], zw[:], z_rows[ci][:, :, k : k + w], w)
-                    woven_z[ci, k] = zw
+        def weigh(g):
+            half, t0 = GROUPS[g]
+            for k in range(PAIR):
+                t = t0 + k
+                if g == WEIGH_ON_SCALAR:
+                    nc.scalar.activation(
+                        z_rows[half][:, t, :], mix[g]["big"][:, k, :], ACT.Copy, scale=gt_c[:, t : t + 1]
+                    )
+                else:
+                    nc.vector.tensor_scalar_mul(z_rows[half][:, t, :], mix[g]["big"][:, k, :], gt_c[:, t : t + 1])
 
-        def mix_product(u):
-            ci, t = mix_units[u]
-            if t == PACK - MG:
-                if ci == 0:
-                    for j in range(PACK):
-                        h_ps.append(psum.tile([P, H], F32, name="h_ps%d" % j, tag="bank%d" % j))
-                c0, n = MIX_CHUNKS[ci]
-                for k, w in pieces(ci, MIX_CHUNKS, SUB):
-                    z_codes = keep.tile([P, w], U32, name="z_codes%d_%d" % (ci, k), align_bytes=64)
-                    z_plane = keep.tile([P, w], U8, name="z_plane%d_%d" % (ci, k), align_bytes=64)
-                    nc.vector.quantize_mx(out=z_codes[:].bitcast(FP8X4), scales=z_plane[:], in_=woven_z[ci, k][:])
-                    for j in range(PACK):
-                        product(h_ps[j][:, c0 + k : c0 + k + w], w1w, w1s, j, z_codes[:], z_plane[:])
-                hw = min(n, HW)
-                for k in range(0, n, hw):
-                    for j in range(PACK):
-                        cols = slice(c0 + k, c0 + k + hw)
-                        copy_on(H_ENG[4 * (ci + k // hw) + j], h_sb[j][:, cols], h_ps[j][:, cols])
+        def weave_z(g):
+            half, t0 = GROUPS[g]
+            if t0 + PAIR == PACK:
+                nc.vector.tensor_copy(*weave(z_woven[half][:], z_rows[half][:]))
 
-        steps = ((look_up, 0), (candidates, 0), (mix_product, MLAGS[3]), (larger, MLAGS[0]), (weigh, MLAGS[1]), (weave_z, MLAGS[2]))
-        for i in range(len(mix_units) + max(MLAGS)):
-            for step, lag in steps:
-                if 0 <= i - lag < len(mix_units):
-                    step(i - lag)
+        def mix_product(g):
+            half, t0 = GROUPS[g]
+            if t0 + PAIR == PACK:
+                if half == 0:
+                    for t in range(PACK):
+                        h_ps.append(psum.tile([P, H], F32, name="h_ps%d" % t, tag="bank%d" % t))
+                cols = half_columns(half)
+                z_codes = keep.tile([P, HALF], U32, name="z_codes%d" % half, align_bytes=64)
+                z_plane = keep.tile([P, HALF], U8, name="z_plane%d" % half, align_bytes=64)
+                nc.vector.quantize_mx(out=z_codes[:].bitcast(FP8X4), scales=z_plane[:], in_=z_woven[half][:])
+                for t in range(PACK):
+                    product(h_ps[t][:, cols], w1_codes, w1_plane, t, z_codes[:], z_plane[:])
+                for t in range(PACK):
+                    copy = nc.vector.tensor_copy if half == 1 and t % 2 == 0 else nc.scalar.copy
+                    copy(h_sb[t][:, cols], h_ps[t][:, cols])
+
+        pipeline(((look_up_d, 0), (candidates, 0), (mix_product, 3), (larger, 0), (weigh, 1), (weave_z, 2)))
 
         out_rows = out_0.rearrange("(p t) j -> p t j", t=PACK)
-        o_codes = keep.tile([P, H], U32, name="o_codes", align_bytes=64)
-        o_plane = keep.tile([P, H], U8, name="o_plane", align_bytes=64)
-        o_words = out_1[0].rearrange("p n t -> p (n t)").bitcast(I32)
-        results = [keep.tile([P, PACK, n], F32, name="result%d" % ci) for ci, (c0, n) in enumerate(OUT_CHUNKS)]
-        units = [(ci, t) for ci in range(len(OUT_CHUNKS)) for t in range(0, PACK, OG)]
-        held = {}
+        out_words = out_1[0].rearrange("p n t -> p (n t)").bitcast(I32)
+        out_codes = keep.tile([P, H], U32, name="out_codes", align_bytes=64)
+        out_plane = keep.tile([P, H], U8, name="out_plane", align_bytes=64)
+        results = [keep.tile([P, PACK, HALF], F32, name="result%d" % half) for half in range(2)]
+        norm = [dict() for g in GROUPS]
+        spread_slot, level_slot = 0, 1
+        taken = [PACK - 1]
 
-        def fetch(u):
-            ci, t0 = units[u]
-            c0, n = OUT_CHUNKS[ci]
-            pa = ring.tile([P, OG, n], F32, name="pa", bufs=FB)
-            pb = ring.tile([P, OG, n], F32, name="pb", bufs=FB)
-            for g in range(OG):
-                t = t0 + g
-                gather_on(PA_ENG[4 * ci + t], pa[:, g, :], h_sb[t], n3_l, c0, n, FETCH)
-                gather_on(PB_ENG[4 * ci + t], pb[:, g, :], h_sb[t], n4_l, c0, n, -FETCH)
-            held[u] = dict(pa=pa, pb=pb)
+        def next_bank():
+            taken.append((taken[-1] + 1) % BANKS)
+            return "bank%d" % taken[-1]
 
-        def both(u):
-            ci, t0 = units[u]
-            c0, n = OUT_CHUNKS[ci]
-            pair = ring.tile([P, OG, n], F32, name="pair", bufs=6)
-            if PG:
-                nc.vector.tensor_tensor(pair[:], held[u]["pb"][:], held[u]["pa"][:], ALU.subtract)
-            else:
-                for g in range(OG):
-                    nc.vector.tensor_tensor(pair[:, g, :], held[u]["pb"][:, g, :], held[u]["pa"][:, g, :], ALU.subtract)
-            held[u]["pair"] = pair
+        def h_part(g, k):
+            half, t0 = GROUPS[g]
+            return h_sb[t0 + k][:, half_columns(half)]
 
-        def numerator(u):
-            ci, t0 = units[u]
-            c0, n = OUT_CHUNKS[ci]
-            num = ring.tile([P, OG, n], F32, name="num", bufs=6)
-            for g in range(OG):
-                nc.vector.scalar_tensor_tensor(
-                    num[:, g, :], held[u]["pair"][:, g, :], 5.0 / 11.0 / FETCH, h_sb[t0 + g][:, c0 : c0 + n],
-                    ALU.mult, ALU.add,
+        def turn(dst, src, b, start, stop):
+            blk = slice(b * P, (b + 1) * P)
+            nc.tensor.matmul(dst[:, blk], src[:, blk], ident[:], start=start, stop=stop, is_transpose=True)
+
+        def fetch(g):
+            half, t0 = GROUPS[g]
+            a, b = group_tile("a"), group_tile("b")
+            for k in range(PAIR):
+                row = h_sb[t0 + k][:]
+                nc.scalar.activation(a[:, k, :], row.indirect(half_entries(n3_l, half)), ACT.Copy, scale=FETCH)
+                nc.vector.tensor_scalar(
+                    b[:, k, :], row.indirect(half_entries(n4_l, half)), -FETCH, 0.0, ALU.mult, ALU.add
                 )
-            held[u]["num"] = num
+            b_less_a = group_tile("b_less_a")
+            nc.vector.tensor_tensor(b_less_a[:], b[:], a[:], ALU.subtract)
+            norm[g]["a"], norm[g]["b"], norm[g]["b_less_a"] = a, b, b_less_a
 
-        def squares(u):
-            ci, t0 = units[u]
-            c0, n = OUT_CHUNKS[ci]
-            sq = ring.tile([P, OG, 2, n], F32, name="sq")
-            held[u]["sq"] = sq
-            for g in range(OG):
-                h_part = h_sb[t0 + g][:, c0 : c0 + n]
-                pa, pb, pair = held[u]["pa"][:, g, :], held[u]["pb"][:, g, :], held[u]["pair"][:, g, :]
-                if MODE[4 * ci + t0] == "v":
-                    forms = ring.tile([P, 2, n], F32, name="forms")
-                    nc.vector.tensor_tensor(forms[:, 0, :], pa, pb, ALU.add)
-                    nc.vector.tensor_tensor(forms[:, 1, :], h_part, pair, ALU.add)
-                    nc.scalar.activation(sq[:, g, :, :], forms[:], ACT.Square)
-                else:
-                    turned = psum.tile([P, 2, n], F32, name="turned", tag=next_bank())
-                    terms = ((1, h_part), (0, pa), (0, pb), (1, pair))
-                    passes = [(half, src, b) for half, src in terms for b in range(n // P)]
-                    for k, (half, src, b) in enumerate(passes):
-                        blk = slice(b * P, (b + 1) * P)
-                        nc.tensor.matmul(
-                            turned[:, half, blk], src[:, blk], ident[:],
-                            start=(k == 0), stop=(k == len(passes) - 1), is_transpose=True,
-                        )
-                    nc.scalar.activation(sq[:, g, 0, :], turned[:, 0, :], ACT.Square, scale=math.sqrt(0.5) / FETCH)
-                    nc.scalar.activation(sq[:, g, 1, :], turned[:, 1, :], ACT.Square, scale=math.sqrt(0.5) * 0.625)
-
-        def inverse_root(u):
-            ci, t0 = units[u]
-            c0, n = OUT_CHUNKS[ci]
-            sq = held[u]["sq"]
-            root = ring.tile([P, OG, n], F32, name="root")
-            held[u]["root"] = root
-            if MODE[4 * ci + t0] == "v":
-                both_sq = ring.tile([P, OG, n], F32, name="both_sq")
+        def numerator(g):
+            num = group_tile("num")
+            for k in range(PAIR):
                 nc.vector.scalar_tensor_tensor(
-                    both_sq[:], sq[:, :, 1, :], (0.625 * FETCH) ** 2, sq[:, :, 0, :], ALU.mult, ALU.add
+                    num[:, k, :], norm[g]["b_less_a"][:, k, :], 5.0 / 11.0 / FETCH, h_part(g, k), ALU.mult, ALU.add
                 )
-                nc.scalar.activation(root[:], both_sq[:], ACT.Abs_reciprocal_sqrt, bias=0.25, scale=0.5 / FETCH**2)
-            else:
-                total = psum.tile([P, OG, n], F32, name="total", tag=next_bank())
-                for g in range(OG):
-                    for b in range(n // P):
-                        blk = slice(b * P, (b + 1) * P)
-                        for k in range(2):
-                            nc.tensor.matmul(
-                                total[:, g, blk], sq[:, g, k, blk], ident[:],
-                                start=(k == 0), stop=(k == 1), is_transpose=True,
-                            )
-                nc.scalar.activation(root[:], total[:], ACT.Abs_reciprocal_sqrt, bias=0.25)
+            norm[g]["num"] = num
 
-        def finish(u):
-            ci, t0 = units[u]
-            c0, n = OUT_CHUNKS[ci]
-            cols = slice(c0, c0 + n)
-            rows = slice(t0, t0 + OG)
+        def squares(g):
+            a, b, b_less_a = norm[g]["a"], norm[g]["b"], norm[g]["b_less_a"]
+            sq = per_group.tile([P, PAIR, 2, HALF], F32, name="sq")
+            norm[g]["sq"] = sq
+            if g == SUMS_ON_VECTOR:
+                forms = keep.tile([P, PAIR, 2, HALF], F32, name="forms")
+                nc.vector.tensor_tensor(forms[:, :, spread_slot, :], a[:], b[:], ALU.add)
+                for k in range(PAIR):
+                    nc.vector.tensor_tensor(forms[:, k, level_slot, :], h_part(g, k), b_less_a[:, k, :], ALU.add)
+                nc.scalar.activation(sq[:], forms[:], ACT.Square)
+            else:
+                level_terms = [[h_part(g, k) for k in range(PAIR)], [b_less_a[:, k, :] for k in range(PAIR)]]
+                spread_terms = [[a[:, k, :] for k in range(PAIR)], [b[:, k, :] for k in range(PAIR)]]
+                for slot, terms, factor in ((level_slot, level_terms, 0.625), (spread_slot, spread_terms, 1.0 / FETCH)):
+                    turned = psum.tile([P, PAIR, HALF], F32, name="turned", tag=next_bank())
+                    passes = [(k, term[k], blk) for term in terms for k in range(PAIR) for blk in range(HALF // P)]
+                    for i, (k, src, blk) in enumerate(passes):
+                        turn(turned[:, k, :], src, blk, i == 0, i == len(passes) - 1)
+                    nc.scalar.activation(sq[:, :, slot, :], turned[:], ACT.Square, scale=math.sqrt(0.5) * factor)
+
+        def inverse_root(g):
+            sq = norm[g]["sq"]
+            root = group_tile("root")
+            norm[g]["root"] = root
+            if g == SUMS_ON_VECTOR:
+                total = keep.tile([P, PAIR, HALF], F32, name="total")
+                nc.vector.scalar_tensor_tensor(
+                    total[:], sq[:, :, level_slot, :], (0.625 * FETCH) ** 2, sq[:, :, spread_slot, :], ALU.mult, ALU.add
+                )
+                nc.scalar.activation(root[:], total[:], ACT.Abs_reciprocal_sqrt, bias=0.25, scale=0.5 / FETCH**2)
+            else:
+                total_ps = psum.tile([P, PAIR, HALF], F32, name="total_ps", tag=next_bank())
+                for k in range(PAIR):
+                    for blk in range(HALF // P):
+                        turn(total_ps[:, k, :], sq[:, k, spread_slot, :], blk, True, False)
+                        turn(total_ps[:, k, :], sq[:, k, level_slot, :], blk, False, True)
+                nc.scalar.activation(root[:], total_ps[:], ACT.Abs_reciprocal_sqrt, bias=0.25)
+
+        def finish(g):
+            half, t0 = GROUPS[g]
+            cols, rows = half_columns(half), slice(t0, t0 + PAIR)
             nc.vector.scalar_tensor_tensor(
-                results[ci][:, rows, :], held[u]["num"][:], 0.6875, held[u]["root"][:], ALU.mult, ALU.mult
+                results[half][:, rows, :], norm[g]["num"][:], 0.6875, norm[g]["root"][:], ALU.mult, ALU.mult
             )
-            nc.sync.dma_start(out=out_rows[:, rows, cols], in_=results[ci][:, rows, :])
-            if t0 == PACK - OG:
-                parts = []
-                for k, w in pieces(ci, OUT_CHUNKS, OSUB):
-                    o_woven = keep.tile([P, PACK * w], BF16, name="o_woven%d_%d" % (ci, k), align_bytes=64)
-                    weave_on(OW_ENG[ci + k // w], o_woven[:], results[ci][:, :, k : k + w], w)
-                    parts.append((slice(c0 + k, c0 + k + w), o_woven))
-                for part, o_woven in parts:
-                    nc.vector.quantize_mx(out=o_codes[:, part].bitcast(FP8X4), scales=o_plane[:, part], in_=o_woven[:])
-                nc.sync.dma_start(out=o_words[:, cols], in_=o_codes[:, cols].bitcast(I32))
+            nc.sync.dma_start(out=out_rows[:, rows, cols], in_=results[half][:, rows, :])
+            if t0 + PAIR == PACK:
+                if half == 0:
+                    shares = ((0, HALF, nc.scalar.copy),)
+                else:
+                    shares = ((0, P, nc.vector.tensor_copy), (P, P, nc.scalar.copy))
+                woven = []
+                for first, width, copy in shares:
+                    part = keep.tile([P, PACK * width], BF16, name="out_woven%d_%d" % (half, first), align_bytes=64)
+                    copy(*weave(part[:], results[half][:, :, first : first + width]))
+                    woven.append((slice(cols.start + first, cols.start + first + width), part))
+                for part_cols, part in woven:
+                    nc.vector.quantize_mx(
+                        out=out_codes[:, part_cols].bitcast(FP8X4), scales=out_plane[:, part_cols], in_=part[:]
+                    )
+                nc.sync.dma_start(out=out_words[:, cols], in_=out_codes[:, cols].bitcast(I32))
 
-        steps = ((fetch, 0), (both, LAGS[0]), (finish, LAGS[1]), (numerator, LAGS[2]), (squares, LAGS[3]), (inverse_root, LAGS[4]))
-        for i in range(len(units) + max(LAGS)):
-            for step, lag in steps:
-                if 0 <= i - lag < len(units):
-                    step(i - lag)
+        last = len(GROUPS) - 1
+        pipeline(((fetch, 0), (finish, last + 1), (numerator, last), (squares, 1), (inverse_root, last)))
+
         for q in range(4):
             queue = nc.sync if q % 2 == 0 else nc.scalar
             queue.dma_start(
-                out=out_2[0, 4 * q : 4 * q + 4, :].bitcast(I32), in_=o_plane[32 * q : 32 * q + 4, :].bitcast(I32)
+                out=out_2[0, 4 * q : 4 * q + 4, :].bitcast(I32), in_=out_plane[32 * q : 32 * q + 4, :].bitcast(I32)
             )

import math
from contextlib import ExitStack

import concourse.mybir as mybir
from concourse.masks import make_identity

T, S, H, N = 2048, 512, 512, 512
FLOPS = 3 * 2 * 512 * 512 * 512

F32 = mybir.dt.float32
BF16 = mybir.dt.bfloat16
I32 = mybir.dt.int32
U32 = mybir.dt.uint32
U16 = mybir.dt.uint16
U8 = mybir.dt.uint8
FP8X4 = mybir.dt.float8_e4m3fn_x4
ALU = mybir.AluOpType
ACT = mybir.ActivationFunctionType

P = 128
PACK = 4
HALF = 256
PAIR = 2
BANKS = 8
GROUPS = [(half, t0) for half in range(2) for t0 in range(0, PACK, PAIR)]

N2_ON_VECTOR = 3
WEIGH_ON_SCALAR = 2
SUMS_ON_VECTOR = 1

FETCH = 0.6


def weave(dst, src):
    return (
        dst.rearrange("p (c i t) -> p c t i", i=4, t=PACK),
        src.rearrange("p t (c i) -> p c t i", i=4),
    )


def deal(dst, src):
    return dst.rearrange("p (t m) -> p t m", t=PACK), src.rearrange("p (m t) -> p t m", t=PACK)


def half_columns(half):
    return slice(half * HALF, (half + 1) * HALF)


def half_entries(lst, half):
    return lst[:, half * HALF // 16 : (half + 1) * HALF // 16]


def pipeline(steps):
    for i in range(len(GROUPS) + max(lag for step, lag in steps)):
        for step, lag in steps:
            if 0 <= i - lag < len(GROUPS):
                step(i - lag)


def tile_picked_twtmxbstd_none_po_kernel(
    tc, x_words, x_scales, wa, wb, sl, th, gt, w1_words, w1_scales, offs, two, n1, n2, n3, n4, out_0, out_1, out_2
):
    nc = tc.nc
    with ExitStack() as ctx:
        keep = ctx.enter_context(tc.tile_pool(name="keep", bufs=1))
        per_group = ctx.enter_context(tc.tile_pool(name="per_group", bufs=len(GROUPS)))
        psum = ctx.enter_context(tc.psum_pool(name="psum", bufs=1))

        def load_list(src, name):
            lst = keep.tile([P, S // 16], U16, name=name)
            nc.sync.dma_start(lst[:], src)
            return lst

        def load_words(src, width, name):
            words = keep.tile([P, width], U32, name=name, align_bytes=64)
            nc.sync.dma_start(out=words[:].bitcast(I32), in_=src[0].rearrange("p n t -> p (n t)").bitcast(I32))
            return words

        def load_column(src, name):
            col = keep.tile([P, PACK], F32, name=name)
            nc.sync.dma_start(out=col[:], in_=src.rearrange("(p t) o -> p (t o)", t=PACK))
            return col

        def load_weight(w, cols, name):
            raw = keep.tile([P, PACK, cols.stop - cols.start], F32, name=name)
            nc.sync.dma_start(out=raw[:], in_=w.rearrange("(p j) c -> p j c", j=PACK)[:, :, cols])
            return raw

        x_plane = keep.tile([P, T], U8, name="x_plane", align_bytes=64)
        w1_plane_raw = keep.tile([P, N], U8, name="w1_plane_raw", align_bytes=64)
        nc.gpsimd.memset(w1_plane_raw[:].bitcast(I32), 0)
        two_l = load_list(two, "two_l")
        for q in range(4):
            nc.sync.dma_start(
                out=x_plane[32 * q : 32 * q + 32, :].bitcast(I32),
                in_=x_scales[0, 4 * q : 4 * q + 4, :].bitcast(I32).partition_broadcast(8),
            )
        offs_l = load_list(offs, "offs_l")
        wb_raw = load_weight(wb, slice(0, H), "wb_raw")
        x_codes = load_words(x_words, T, "x_codes")
        n1_l = load_list(n1, "n1_l")
        sl_c = load_column(sl, "sl_c")
        th_c = load_column(th, "th_c")
        n2_l = load_list(n2, "n2_l")
        wa_raw = [load_weight(wa, half_columns(half), "wa_raw%d" % half) for half in range(2)]
        w1_codes_raw = load_words(w1_words, N, "w1_codes_raw")
        gt_c = load_column(gt, "gt_c")
        for q in range(4):
            nc.sync.dma_start(
                out=w1_plane_raw[32 * q : 32 * q + 4, :].bitcast(I32),
                in_=w1_scales[0, 4 * q : 4 * q + 4, :].bitcast(I32),
            )
        n3_l = load_list(n3, "n3_l")
        n4_l = load_list(n4, "n4_l")
        ident = keep.tile([P, P], F32, name="ident")
        make_identity(nc, ident[:])

        def pick(window, lst, dtype, name):
            picked = keep.tile([P, S], dtype, name=name, align_bytes=64)
            nc.vector.tensor_copy(picked[:].rearrange("p (t m) -> p m t", t=PACK), window[:].indirect(lst[:]))
            return picked

        def quantise_weight(halves, name):
            codes = keep.tile([P, H], U32, name=name + "_codes", align_bytes=64)
            plane = keep.tile([P, H], U8, name=name + "_plane", align_bytes=64)
            for half in range(2):
                woven = keep.tile([P, PACK * HALF], BF16, name=name + "_woven%d" % half, align_bytes=64)
                nc.vector.tensor_copy(*weave(woven[:], halves[half]))
                cols = half_columns(half)
                nc.vector.quantize_mx(out=codes[:, cols].bitcast(FP8X4), scales=plane[:, cols], in_=woven[:])
            return codes, plane

        def product(result, lhs_codes, lhs_plane, t, rhs_codes, rhs_plane):
            cols = slice(t * P, (t + 1) * P)
            nc.tensor.matmul_mx(
                out=result,
                lhsT=lhs_codes[:, cols].bitcast(FP8X4),
                lhsT_scale=lhs_plane[:, cols],
                rhs=rhs_codes.bitcast(FP8X4),
                rhs_scale=rhs_plane,
                start=True,
                stop=True,
            )

        two_plane = pick(x_plane, two_l, U8, "two_plane")
        offs_plane = pick(x_plane, offs_l, U8, "offs_plane")
        wb_codes, wb_plane = quantise_weight([wb_raw[:, :, half_columns(half)] for half in range(2)], "wb")
        two_codes = pick(x_codes, two_l, U32, "two_codes")
        d_ps = [psum.tile([P, H], F32, name="d_ps%d" % t, tag="bank%d" % t) for t in range(PACK)]
        d_sb = [keep.tile([P, H], F32, name="d_sb%d" % t) for t in range(PACK)]
        for t in range(PACK):
            product(d_ps[t][:], two_codes, two_plane, t, wb_codes[:], wb_plane[:])
        offs_codes = pick(x_codes, offs_l, U32, "offs_codes")

        sl_th = keep.tile([P, PACK], F32, name="sl_th")
        sg_bias = keep.tile([P, PACK], F32, name="sg_bias")
        nc.gpsimd.tensor_tensor(sl_th[:], sl_c[:], th_c[:], ALU.mult)
        nc.gpsimd.tensor_scalar(sg_bias[:], sl_th[:], -1.0, 0.0, ALU.mult, ALU.add)

        wa_codes, wa_plane = quantise_weight([raw[:] for raw in wa_raw], "wa")
        y_ps = [psum.tile([P, PAIR, HALF], F32, name="y_ps%d" % g, tag="bank%d" % (PACK + g)) for g in range(len(GROUPS))]
        for g, (half, t0) in enumerate(GROUPS):
            cols = half_columns(half)
            for k in range(PAIR):
                product(y_ps[g][:, k, :], offs_codes, offs_plane, t0 + k, wa_codes[:, cols], wa_plane[:, cols])

        w1_codes = keep.tile([P, N], U32, name="w1_codes", align_bytes=64)
        nc.vector.tensor_copy(*deal(w1_codes[:], w1_codes_raw[:]))
        w1_plane = keep.tile([P, N], U8, name="w1_plane", align_bytes=64)
        nc.vector.tensor_copy(*deal(w1_plane[:], w1_plane_raw[:]))

        h_ps = []
        h_sb = [keep.tile([P, H], F32, name="h_sb%d" % t) for t in range(PACK)]
        z_rows = [keep.tile([P, PACK, HALF], BF16, name="z_rows%d" % half) for half in range(2)]
        z_woven = [keep.tile([P, PACK * HALF], BF16, name="z_woven%d" % half, align_bytes=64) for half in range(2)]
        mix = [dict() for g in GROUPS]

        def group_tile(name):
            return per_group.tile([P, PAIR, HALF], F32, name=name)

        def look_up_d(g):
            half, t0 = GROUPS[g]
            sg, d2 = group_tile("sg"), group_tile("d2")
            for k in range(PAIR):
                t = t0 + k
                if half == 0:
                    nc.scalar.copy(d_sb[t][:], d_ps[t][:])
                nc.scalar.activation(
                    sg[:, k, :], d_sb[t][:].indirect(half_entries(n1_l, half)), ACT.Sigmoid,
                    bias=sg_bias[:, t : t + 1], scale=sl_c[:, t : t + 1],
                )
                by_n2 = d_sb[t][:].indirect(half_entries(n2_l, half))
                if PAIR * g + k < N2_ON_VECTOR:
                    nc.vector.tensor_copy(d2[:, k, :], by_n2)
                else:
                    nc.scalar.activation(d2[:, k, :], by_n2, ACT.Copy)
            if g == len(GROUPS) - 1:
                warm = keep.tile([P, 1], F32, name="warm")
                nc.scalar.activation(warm[:], sg[:, PAIR - 1, 0:1], ACT.Abs_reciprocal_sqrt, bias=0.25)
            mix[g]["sg"], mix[g]["d2"] = sg, d2

        def candidates(g):
            half, t0 = GROUPS[g]
            diff, gated = group_tile("diff"), group_tile("gated")
            for k in range(PAIR):
                own = d_sb[t0 + k][:, half_columns(half)]
                nc.vector.tensor_tensor(diff[:, k, :], mix[g]["d2"][:, k, :], own, ALU.subtract)
            nc.vector.tensor_tensor(gated[:], y_ps[g][:], mix[g]["sg"][:], ALU.mult)
            mix[g]["diff"], mix[g]["gated"] = diff, gated

        def larger(g):
            big = group_tile("big")
            nc.vector.tensor_tensor(big[:], mix[g]["gated"][:], mix[g]["diff"][:], ALU.max)
            mix[g]["big"] = big

        def weigh(g):
            half, t0 = GROUPS[g]
            for k in range(PAIR):
                t = t0 + k
                if g == WEIGH_ON_SCALAR:
                    nc.scalar.activation(
                        z_rows[half][:, t, :], mix[g]["big"][:, k, :], ACT.Copy, scale=gt_c[:, t : t + 1]
                    )
                else:
                    nc.vector.tensor_scalar_mul(z_rows[half][:, t, :], mix[g]["big"][:, k, :], gt_c[:, t : t + 1])

        def weave_z(g):
            half, t0 = GROUPS[g]
            if t0 + PAIR == PACK:
                nc.vector.tensor_copy(*weave(z_woven[half][:], z_rows[half][:]))

        def mix_product(g):
            half, t0 = GROUPS[g]
            if t0 + PAIR == PACK:
                if half == 0:
                    for t in range(PACK):
                        h_ps.append(psum.tile([P, H], F32, name="h_ps%d" % t, tag="bank%d" % t))
                cols = half_columns(half)
                z_codes = keep.tile([P, HALF], U32, name="z_codes%d" % half, align_bytes=64)
                z_plane = keep.tile([P, HALF], U8, name="z_plane%d" % half, align_bytes=64)
                nc.vector.quantize_mx(out=z_codes[:].bitcast(FP8X4), scales=z_plane[:], in_=z_woven[half][:])
                for t in range(PACK):
                    product(h_ps[t][:, cols], w1_codes, w1_plane, t, z_codes[:], z_plane[:])
                for t in range(PACK):
                    copy = nc.vector.tensor_copy if half == 1 and t % 2 == 0 else nc.scalar.copy
                    copy(h_sb[t][:, cols], h_ps[t][:, cols])

        pipeline(((look_up_d, 0), (candidates, 0), (mix_product, 3), (larger, 0), (weigh, 1), (weave_z, 2)))

        out_rows = out_0.rearrange("(p t) j -> p t j", t=PACK)
        out_words = out_1[0].rearrange("p n t -> p (n t)").bitcast(I32)
        out_codes = keep.tile([P, H], U32, name="out_codes", align_bytes=64)
        out_plane = keep.tile([P, H], U8, name="out_plane", align_bytes=64)
        results = [keep.tile([P, PACK, HALF], F32, name="result%d" % half) for half in range(2)]
        norm = [dict() for g in GROUPS]
        spread_slot, level_slot = 0, 1
        taken = [PACK - 1]

        def next_bank():
            taken.append((taken[-1] + 1) % BANKS)
            return "bank%d" % taken[-1]

        def h_part(g, k):
            half, t0 = GROUPS[g]
            return h_sb[t0 + k][:, half_columns(half)]

        def turn(dst, src, b, start, stop):
            blk = slice(b * P, (b + 1) * P)
            nc.tensor.matmul(dst[:, blk], src[:, blk], ident[:], start=start, stop=stop, is_transpose=True)

        def fetch(g):
            half, t0 = GROUPS[g]
            a, b = group_tile("a"), group_tile("b")
            for k in range(PAIR):
                row = h_sb[t0 + k][:]
                nc.scalar.activation(a[:, k, :], row.indirect(half_entries(n3_l, half)), ACT.Copy, scale=FETCH)
                nc.vector.tensor_scalar(
                    b[:, k, :], row.indirect(half_entries(n4_l, half)), -FETCH, 0.0, ALU.mult, ALU.add
                )
            b_less_a = group_tile("b_less_a")
            nc.vector.tensor_tensor(b_less_a[:], b[:], a[:], ALU.subtract)
            norm[g]["a"], norm[g]["b"], norm[g]["b_less_a"] = a, b, b_less_a

        def numerator(g):
            num = group_tile("num")
            for k in range(PAIR):
                nc.vector.scalar_tensor_tensor(
                    num[:, k, :], norm[g]["b_less_a"][:, k, :], 5.0 / 11.0 / FETCH, h_part(g, k), ALU.mult, ALU.add
                )
            norm[g]["num"] = num

        def squares(g):
            a, b, b_less_a = norm[g]["a"], norm[g]["b"], norm[g]["b_less_a"]
            sq = per_group.tile([P, PAIR, 2, HALF], F32, name="sq")
            norm[g]["sq"] = sq
            if g == SUMS_ON_VECTOR:
                forms = keep.tile([P, PAIR, 2, HALF], F32, name="forms")
                nc.vector.tensor_tensor(forms[:, :, spread_slot, :], a[:], b[:], ALU.add)
                for k in range(PAIR):
                    nc.vector.tensor_tensor(forms[:, k, level_slot, :], h_part(g, k), b_less_a[:, k, :], ALU.add)
                nc.scalar.activation(sq[:], forms[:], ACT.Square)
            else:
                level_terms = [[h_part(g, k) for k in range(PAIR)], [b_less_a[:, k, :] for k in range(PAIR)]]
                spread_terms = [[a[:, k, :] for k in range(PAIR)], [b[:, k, :] for k in range(PAIR)]]
                for slot, terms, factor in ((level_slot, level_terms, 0.625), (spread_slot, spread_terms, 1.0 / FETCH)):
                    turned = psum.tile([P, PAIR, HALF], F32, name="turned", tag=next_bank())
                    passes = [(k, term[k], blk) for term in terms for k in range(PAIR) for blk in range(HALF // P)]
                    for i, (k, src, blk) in enumerate(passes):
                        turn(turned[:, k, :], src, blk, i == 0, i == len(passes) - 1)
                    nc.scalar.activation(sq[:, :, slot, :], turned[:], ACT.Square, scale=math.sqrt(0.5) * factor)

        def inverse_root(g):
            sq = norm[g]["sq"]
            root = group_tile("root")
            norm[g]["root"] = root
            if g == SUMS_ON_VECTOR:
                total = keep.tile([P, PAIR, HALF], F32, name="total")
                nc.vector.scalar_tensor_tensor(
                    total[:], sq[:, :, level_slot, :], (0.625 * FETCH) ** 2, sq[:, :, spread_slot, :], ALU.mult, ALU.add
                )
                nc.scalar.activation(root[:], total[:], ACT.Abs_reciprocal_sqrt, bias=0.25, scale=0.5 / FETCH**2)
            else:
                total_ps = psum.tile([P, PAIR, HALF], F32, name="total_ps", tag=next_bank())
                for k in range(PAIR):
                    for blk in range(HALF // P):
                        turn(total_ps[:, k, :], sq[:, k, spread_slot, :], blk, True, False)
                        turn(total_ps[:, k, :], sq[:, k, level_slot, :], blk, False, True)
                nc.scalar.activation(root[:], total_ps[:], ACT.Abs_reciprocal_sqrt, bias=0.25)

        def finish(g):
            half, t0 = GROUPS[g]
            cols, rows = half_columns(half), slice(t0, t0 + PAIR)
            nc.vector.scalar_tensor_tensor(
                results[half][:, rows, :], norm[g]["num"][:], 0.6875, norm[g]["root"][:], ALU.mult, ALU.mult
            )
            nc.sync.dma_start(out=out_rows[:, rows, cols], in_=results[half][:, rows, :])
            if t0 + PAIR == PACK:
                if half == 0:
                    shares = ((0, HALF, nc.scalar.copy),)
                else:
                    shares = ((0, P, nc.vector.tensor_copy), (P, P, nc.scalar.copy))
                woven = []
                for first, width, copy in shares:
                    part = keep.tile([P, PACK * width], BF16, name="out_woven%d_%d" % (half, first), align_bytes=64)
                    copy(*weave(part[:], results[half][:, :, first : first + width]))
                    woven.append((slice(cols.start + first, cols.start + first + width), part))
                for part_cols, part in woven:
                    nc.vector.quantize_mx(
                        out=out_codes[:, part_cols].bitcast(FP8X4), scales=out_plane[:, part_cols], in_=part[:]
                    )
                nc.sync.dma_start(out=out_words[:, cols], in_=out_codes[:, cols].bitcast(I32))

        last = len(GROUPS) - 1
        pipeline(((fetch, 0), (finish, last + 1), (numerator, last), (squares, 1), (inverse_root, last)))

        for q in range(4):
            queue = nc.sync if q % 2 == 0 else nc.scalar
            queue.dma_start(
                out=out_2[0, 4 * q : 4 * q + 4, :].bitcast(I32), in_=out_plane[32 * q : 32 * q + 4, :].bitcast(I32)
            )
